import numpy as np
import ml_dtypes


def mxq(x, axis, fmt="e4m3"):
    dtype, down = {"e4m3": (ml_dtypes.float8_e4m3fn, 7), "e5m2": (ml_dtypes.float8_e5m2, 14)}[fmt]
    v = np.moveaxis(np.asarray(x, np.float32).astype(ml_dtypes.bfloat16).astype(np.float64), axis, -1)
    blocks = v.reshape(v.shape[:-1] + (-1, 32))
    amax = np.abs(blocks).max(-1, keepdims=True)
    byte = np.maximum(np.where(amax > 0, np.frexp(amax)[1] - 1 + 127, 0) - down, 1)
    scale = np.exp2(byte - 127.0)
    codes = (blocks / scale).astype(np.float32).astype(dtype).astype(np.float64)
    return np.moveaxis((codes * scale).reshape(v.shape), -1, axis)


WIDE = False


def mx_kscale(k):
    if not WIDE:
        return np.ones(k)
    levels = np.array([10, -10, 5, -5, 0])
    if k % 512:
        return np.exp2(np.random.permutation(np.resize(levels, k // 32))).repeat(32)
    a = np.empty((k // 512, 16))
    for p in range(k // 512):
        a[p, :8] = np.random.permutation(np.resize(levels, 8))
        for g in range(8):
            far = levels[np.abs(levels - a[p, g]) >= 10]
            a[p, g + 8] = far[np.random.randint(len(far))]
    return np.exp2(a.ravel()).repeat(32)


BF16 = ml_dtypes.bfloat16


def bf(x):
    return np.asarray(x, np.float32).astype(BF16)


def f64(x):
    return np.asarray(x).astype(np.float64)


E2M1 = np.array([0.0, 0.5, 1.0, 1.5, 2.0, 3.0, 4.0, 6.0, -0.0, -0.5, -1.0, -1.5, -2.0, -3.0, -4.0, -6.0])


def pack_weight(w, fmt):
    k, n = w.shape
    w = f64(bf(w)).reshape(k // 32, 32, n)
    amax = np.abs(w).max(1)
    if fmt == "e4m3":
        byte = np.frexp(amax)[1] - 1 + 127 - 7
    else:
        mant, ex = np.frexp(amax / 6.0)
        byte = np.where(mant > 0.5, ex, ex - 1) + 127
    byte = np.clip(np.where(amax > 0, byte, 1), 1, 254)
    scaled = (w * np.exp2(127.0 - byte)[:, None, :]).reshape(k, n).astype(np.float32)
    by_word = np.ascontiguousarray(scaled.reshape(k // 512, 128, 4, n).transpose(0, 1, 3, 2))
    if fmt == "e4m3":
        words = by_word.astype(ml_dtypes.float8_e4m3fn).view(np.uint8)
    else:
        c = by_word.astype(ml_dtypes.float4_e2m1fn).view(np.uint8) & 0xF
        words = c[..., 0::2] | (c[..., 1::2] << 4)
    return np.ascontiguousarray(words), np.ascontiguousarray(byte.astype(np.uint8).reshape(k // 512, 16, n))


def unpack_weight(words, scales, fmt):
    g, p, n, _ = words.shape
    if fmt == "e4m3":
        vals = np.ascontiguousarray(words).view(ml_dtypes.float8_e4m3fn).astype(np.float64)
    else:
        nib = np.empty((g, p, n, 4), np.uint8)
        nib[..., 0::2] = words & 0xF
        nib[..., 1::2] = words >> 4
        vals = E2M1[nib]
    vals = vals * np.repeat(np.exp2(scales.astype(np.float64) - 127.0), 8, axis=1)[..., None]
    return vals.transpose(0, 1, 3, 2).reshape(g * 512, n)

E4M3FN = np.array([(-1.0 if i & 128 else 1.0) * ((1.0 + (i & 7) / 8.0) * 2.0 ** (((i >> 3) & 15) - 7) if i & 120 else (i & 7) * 2.0 ** -9) for i in range(256)])


def e4m3fn_bytes(y):
    return np.clip(np.asarray(y, np.float64), -448.0, 448.0).astype(np.float32).astype(ml_dtypes.float8_e4m3fn).view(np.uint8)


def e4m3fn_values(b):
    return E4M3FN[b]


B, S, D, R = 1, 1024, 512, 512


def sketch_features(xq, g1q, g2q, scale):
    return (xq @ g1q) * (xq @ g2q) * scale


def draw0():
    s, t = mx_kscale(D), mx_kscale(R)
    q = bf(np.random.standard_normal((B, S, D)) * s)
    k = bf(np.random.standard_normal((B, S, D)) * s)
    g1_words, g1_scales = pack_weight(np.random.standard_normal((D, R)) / np.sqrt(D) / s[:, None], "e4m3")
    g2_words, g2_scales = pack_weight(np.random.standard_normal((D, R)) / np.sqrt(D) / s[:, None], "e4m3")
    return {
        "q": q,
        "k": k,
        "g1_words": g1_words,
        "g1_scales": g1_scales,
        "g2_words": g2_words,
        "g2_scales": g2_scales,
        "a": bf((1.0 + 0.1 * np.random.standard_normal(R)) * t),
        "b": bf((1.0 + 0.1 * np.random.standard_normal(R)) / t),
    }


def core(q, k, g1_words, g1_scales, g2_words, g2_scales, a, b):
    n = q.shape[1]
    g1q = unpack_weight(g1_words, g1_scales, "e4m3")
    g2q = unpack_weight(g2_words, g2_scales, "e4m3")
    r = g1q.shape[1]
    fq = sketch_features(mxq(f64(q), 2, "e4m3"), g1q, g2q, f64(a))
    fk = sketch_features(mxq(f64(k), 2, "e4m3"), g1q, g2q, f64(b))
    z = (mxq(fq, 2, "e4m3") @ mxq(fk, 2, "e4m3").transpose(0, 2, 1)) / np.sqrt(r)
    rows = np.arange(n)[:, None]
    cols = np.arange(n)[None, :]
    l = np.where((cols <= rows)[None, :, :], z * z, 0.0)
    den = 1.0 + (1.0 / n) * np.sum(l, axis=-1)
    return l / den[:, :, None]


def setup_inputs():
    drawn = draw0()
    full = np.asarray(drawn['q']).astype(np.float64)
    scale = (np.abs(full).reshape(1, 1024, 4, 128).max(axis=(3,)) / 448.0).astype(np.float32)
    given = {}
    for key, value in drawn.items():
        if key == 'q':
            given['q_bytes'] = e4m3fn_bytes(full / np.repeat(scale.astype(np.float64), 128, axis=2))
            given['q_scale'] = scale
        else:
            given[key] = value
    return given


def reference(q_bytes, q_scale, k, g1_words, g1_scales, g2_words, g2_scales, a, b):
    return core(e4m3fn_values(q_bytes) * np.repeat(q_scale.astype(np.float64), 128, axis=2), k, g1_words, g1_scales, g2_words, g2_scales, a, b)

@@ -1,0 +1,360 @@
+import concourse.mybir as mybir
+from concourse.masks import make_identity
+
+S, D, R = 1024, 512, 512
+P = 128
+PAIR = 256
+
+F32 = mybir.dt.float32
+BF16 = mybir.dt.bfloat16
+I32 = mybir.dt.int32
+U32 = mybir.dt.uint32
+U8 = mybir.dt.uint8
+FP8 = mybir.dt.float8_e4m3fn
+FP8X4 = mybir.dt.float8_e4m3fn_x4
+ALU = mybir.AluOpType
+ACT = mybir.ActivationFunctionType
+
+FLOPS = 4 * 2 * S * D * R + 2 * R * (S * (S + 1) // 2)
+
+
+def tile_polysketchdegreefourcausalweights_d1p_kernel(
+    tc, q_bytes, q_scale, k, g1_words, g1_scales, g2_words, g2_scales, a, b, out
+):
+    nc = tc.nc
+    with tc.tile_pool(name="keep", bufs=1) as keep, tc.psum_pool(name="banks", bufs=2) as psum, tc.manual_schedule():
+
+        def sb(name, shape, dtype):
+            return keep.tile(shape, dtype, name=name, align_bytes=64)
+
+        def bank(name, tag, bufs):
+            return psum.tile([P, 512], F32, name=name, tag=tag, bufs=bufs)
+
+        ident = sb("ident", [P, P], F32)
+        ident_b = sb("ident_b", [P, P], BF16)
+        mask = sb("mask", [P, P + 4], F32)
+        zeros = sb("zeros", [P, S - P], F32)
+        ab_rows = sb("ab_rows", [P, P], BF16)
+        ab = sb("ab", [P, 8], F32)
+        s_raw = [sb("s_raw1", [P, P], I32), sb("s_raw2", [P, P], I32)]
+        s_w = [sb("s_w1", [P, P], I32), sb("s_w2", [P, P], I32)]
+        w_raw = [sb("w_raw1", [P, R], I32), sb("w_raw2", [P, R], I32)]
+        w = [sb("w1", [P, R], I32), sb("w2", [P, R], I32)]
+        k_raw = [sb("k_raw%d" % i, [P, 2, D], BF16) for i in range(4)]
+        q_codes8 = [sb("q_lo", [P, 4, D], U8), sb("q_hi", [P, 4, D], U8)]
+        qs = sb("qs", [P, 8, 4], F32)
+        q_bf = [sb("q_bf%d" % i, [P, 2, D], BF16) for i in range(4)]
+        grouped = [sb("grouped%d" % i, [P, 4 * PAIR], BF16) for i in range(8)]
+        codes = [sb("codes%d" % i, [P, PAIR], U32) for i in range(8)]
+        scales = [sb("scales%d" % i, [P, PAIR], U8) for i in range(8)]
+        s1 = [sb("s1_%d" % i, [P, 4, PAIR], F32) for i in range(8)]
+        feat = [sb("feat%d" % i, [P, 4 * PAIR], BF16) for i in range(8)]
+        fk_codes = sb("fk_codes", [P, S], U32)
+        fk_scales = sb("fk_scales", [P, S], U8)
+        fq_codes = [sb("fq_codes%d" % i, [P, PAIR], U32) for i in range(4)]
+        fq_scales = [sb("fq_scales%d" % i, [P, PAIR], U8) for i in range(4)]
+        rows = [sb("row%d" % i, [P, P * (i + 1) + 4], F32) for i in range(8)]
+        den = sb("den", [P, 8], F32)
+        rec = sb("rec", [P, 8], F32)
+
+        nc.vector.memset(s_raw[0][:], 0)
+        nc.vector.memset(ab_rows[:], 0.0)
+        nc.vector.memset(s_raw[1][:], 0)
+        make_identity(nc, ident[:])
+        nc.scalar.copy(out=ident_b[:], in_=ident[:])
+
+        k_view = k[0].rearrange("(i p) d -> p i d", p=P)
+        q_view = q_bytes[0].rearrange("(i p) d -> p i d", p=P)
+
+        def load_scale_rows(queue, g, src):
+            view = src[0].bitcast(I32).rearrange("(q s) n -> s q n", s=4)
+            for s in range(4):
+                queue.dma_start(out=s_raw[g][s : P : 32, :], in_=view[s])
+
+        def load_words(g, src):
+            nc.sync.dma_start(out=w_raw[g][:], in_=src[0].rearrange("p n t -> p (n t)").bitcast(I32))
+
+        nc.gpsimd.dma_start(out=ab_rows[0:4, :].rearrange("t (a r) -> t a r", r=8), in_=b.rearrange("(a t r) -> t a r", t=4, r=8))
+        nc.gpsimd.dma_start(out=ab_rows[4:8, :].rearrange("t (a r) -> t a r", r=8), in_=a.rearrange("(a t r) -> t a r", t=4, r=8))
+        load_scale_rows(nc.sync, 0, g1_scales)
+        nc.sync.dma_start(out=qs[:], in_=q_scale[0].rearrange("(i p) j -> p i j", p=P))
+        nc.sync.dma_start(out=q_codes8[1][:], in_=q_view[:, 4:8, :])
+        nc.sync.dma_start(out=k_raw[0][:], in_=k_view[:, 0:2, :])
+        load_words(0, g1_words)
+        nc.sync.dma_start(out=k_raw[1][:], in_=k_view[:, 2:4, :])
+        nc.sync.dma_start(out=q_codes8[0][:], in_=q_view[:, 0:4, :])
+        load_words(1, g2_words)
+        nc.sync.dma_start(out=k_raw[2][:], in_=k_view[:, 4:6, :])
+        nc.sync.dma_start(out=k_raw[3][:], in_=k_view[:, 6:8, :])
+        load_scale_rows(nc.sync, 1, g2_scales)
+
+        nc.gpsimd.memset(zeros[:], 0.0)
+        for i in range(7):
+            wid = P * (i + 1)
+            nc.sync.dma_start(out=out[0, P * i : P * (i + 1), wid:S], in_=zeros[:, 0 : S - wid])
+        nc.gpsimd.memset(mask[:], 1.0)
+        nc.gpsimd.affine_select(
+            out=mask[:, 0:P], in_=mask[:, 0:P], pattern=[[-1, P]], compare_op=ALU.is_ge, fill=0.0, base=0, channel_multiplier=1
+        )
+        for i in range(8):
+            nc.gpsimd.memset(rows[i][:, P * (i + 1) : P * (i + 1) + 1], 1024.0 * 512.0)
+
+        def k_words(pair):
+            return k_raw[pair][:].rearrange("p i d -> p (i d)").bitcast(F32)
+
+        Q_PAIRS = [3, 2, 1, 0]
+        state = {}
+
+        def is_q(p):
+            return p >= 4
+
+        def token_pair(p):
+            return Q_PAIRS[p - 4] if is_q(p) else p
+
+        def widen(p, engine, first=0, last=8):
+            tp = token_pair(p)
+            for n in range(first, last):
+                if True:
+                    j, blk = n // 4, n % 4
+                    i = 2 * tp + j
+                    src = q_codes8[i // 4][:, i % 4, P * blk : P * (blk + 1)].bitcast(FP8)
+                    dst = q_bf[tp][:, j, P * blk : P * (blk + 1)]
+                    sc = qs[:, i, blk : blk + 1]
+                    if engine == "v":
+                        nc.vector.tensor_scalar(out=dst, in0=src, scalar1=sc, scalar2=None, op0=ALU.mult)
+                    else:
+                        nc.scalar.activation(out=dst, in_=src, func=ACT.Copy, scale=sc)
+
+        def turn(p):
+            words = q_bf[token_pair(p)][:].rearrange("p i d -> p (i d)").bitcast(F32) if is_q(p) else k_words(p)
+            z = bank("turn%d" % p, "Z", 3)
+            for j in range(2):
+                for u in range(2):
+                    nc.tensor.transpose(
+                        z[:, PAIR * u + P * j : PAIR * u + P * (j + 1)], words[:, 256 * j + u : 256 * (j + 1) : 2], ident[:]
+                    )
+            state["turn", p] = z
+
+        def copy_out(p):
+            z = state["turn", p]
+            nc.scalar.copy(
+                out=grouped[p][:].bitcast(F32).rearrange("p (c u) -> p c u", u=2), in_=z[:].rearrange("p (u c) -> p c u", u=2)
+            )
+
+        def quant(p):
+            nc.vector.quantize_mx(out=codes[p][:].bitcast(FP8X4), scales=scales[p][:], in_=grouped[p][:])
+
+        def permute_weights(g):
+            nc.vector.tensor_copy(
+                out=w[g][:].rearrange("p (t a r) -> p t a r", t=4, r=8), in_=w_raw[g][:].rearrange("p (a t r) -> p t a r", t=4, r=8)
+            )
+            nc.vector.tensor_copy(
+                out=s_w[g][:].rearrange("p (t a r) -> p t a r", t=4, r=2), in_=s_raw[g][:].rearrange("p (a t r) -> p t a r", t=4, r=2)
+            )
+
+        def mx(out_ap, g, t, p, c0, c1):
+            nc.tensor.matmul_mx(
+                out=out_ap,
+                lhsT=w[g][:, P * t : P * (t + 1)].bitcast(FP8X4),
+                lhsT_scale=s_w[g][:].bitcast(U8)[:, P * t : P * (t + 1)],
+                rhs=codes[p][:, c0:c1].bitcast(FP8X4),
+                rhs_scale=scales[p][:, c0:c1],
+                start=True,
+                stop=True,
+            )
+
+        def m1(p, h):
+            z = bank("m1_%d_%d" % (p, h), "A", 3)
+            for e in range(2):
+                mx(z[:, PAIR * e : PAIR * (e + 1)], 0, 2 * h + e, p, 0, PAIR)
+            state["m1", p, h] = z
+
+        def act1(p):
+            base = 4 if is_q(p) else 0
+            for t in range(4):
+                z = state["m1", p, t // 2]
+                e = t % 2
+                nc.scalar.activation(
+                    out=s1[p][:, t, :], in_=z[:, PAIR * e : PAIR * (e + 1)], func=ACT.Copy, scale=ab[:, base + t : base + t + 1]
+                )
+
+        def m2(p, j):
+            z = bank("m2_%d_%d" % (p, j), "B", 2)
+            for t in range(4):
+                mx(z[:, P * t : P * (t + 1)], 1, t, p, P * j, P * (j + 1))
+            state["m2", p, j] = z
+
+        def prod(p, j):
+            nc.vector.tensor_tensor(
+                out=feat[p][:, 512 * j : 512 * (j + 1)].rearrange("p (n t) -> p n t", t=4),
+                in0=state["m2", p, j][:].rearrange("p (t n) -> p n t", t=4),
+                in1=s1[p][:, :, P * j : P * (j + 1)].rearrange("p t n -> p n t"),
+                op=ALU.mult,
+            )
+
+        def fquant(p):
+            tp = token_pair(p)
+            if is_q(p):
+                nc.vector.quantize_mx(out=fq_codes[tp][:].bitcast(FP8X4), scales=fq_scales[tp][:], in_=feat[p][:])
+            else:
+                cols = slice(PAIR * tp, PAIR * (tp + 1))
+                nc.vector.quantize_mx(out=fk_codes[:, cols].bitcast(FP8X4), scales=fk_scales[:, cols], in_=feat[p][:])
+
+        def zrow(i):
+            tp, j = i // 2, i % 2
+            width = P * (i + 1)
+            banks = []
+            for c0 in range(0, width, 512):
+                z = bank("z%d_%d" % (i, c0), "Z", 3)
+                left = min(512, width - c0)
+                x = 0
+                while x < left:
+                    n = 512 if left - x >= 512 else (256 if left - x >= 256 else 128)
+                    nc.tensor.matmul_mx(
+                        out=z[:, x : x + n],
+                        lhsT=fq_codes[tp][:, P * j : P * (j + 1)].bitcast(FP8X4),
+                        lhsT_scale=fq_scales[tp][:, P * j : P * (j + 1)],
+                        rhs=fk_codes[:, c0 + x : c0 + x + n].bitcast(FP8X4),
+                        rhs_scale=fk_scales[:, c0 + x : c0 + x + n],
+                        start=True,
+                        stop=True,
+                    )
+                    x += n
+                banks.append((c0, left, z))
+            state["z", i] = banks
+
+        def squares(i):
+            width = P * (i + 1)
+            row = rows[i]
+            n_acc = 0
+            for c0, left, z in state["z", i]:
+                off = min(left, width - P - c0)
+                if off > 0:
+                    nc.scalar.activation(
+                        out=row[:, c0 : c0 + off],
+                        in_=z[:, 0:off],
+                        func=ACT.Square,
+                        accum_out=row[:, width + 1 + n_acc : width + 2 + n_acc],
+                    )
+                    n_acc += 1
+                if off < left:
+                    nc.scalar.activation(out=row[:, width - P : width], in_=z[:, off:left], func=ACT.Square)
+            state["n_acc", i] = n_acc
+
+        def mask_and_sum(i):
+            width = P * (i + 1)
+            n = 1 + state["n_acc", i]
+            part = rows[i][:, width - P : width + n]
+            nc.vector.scalar_tensor_tensor(
+                out=part, in0=part, scalar=1.0, in1=mask[:, 0 : P + n], op0=ALU.mult, op1=ALU.mult, accum_out=den[:, i : i + 1]
+            )
+
+        def invert(tp):
+            nc.vector.reciprocal(out=rec[:, 2 * tp : 2 * tp + 2], in_=den[:, 2 * tp : 2 * tp + 2])
+
+        def normalise(i, engine="v"):
+            width = P * (i + 1)
+            row = rows[i]
+            if engine == "v":
+                nc.vector.tensor_scalar(
+                    out=row[:, 0:width], in0=row[:, 0:width], scalar1=rec[:, i : i + 1], scalar2=1024.0, op0=ALU.mult, op1=ALU.mult
+                )
+            else:
+                nc.scalar.activation(out=row[:, 0:width], in_=row[:, 0:width], func=ACT.Copy, scale=rec[:, i : i + 1])
+            nc.sync.dma_start(out=out[0, P * i : P * (i + 1), 0:width], in_=row[:, 0:width])
+
+        def times_1024(tp):
+            nc.vector.tensor_scalar(
+                out=rec[:, 2 * tp : 2 * tp + 2], in0=rec[:, 2 * tp : 2 * tp + 2], scalar1=1024.0, scalar2=None, op0=ALU.mult
+            )
+
+        turn(0)
+        widen(4, "v")
+        widen(5, "s", 0, 6)
+        copy_out(0)
+        widen(5, "s", 6, 8)
+        zab = psum.tile([P, P], BF16, name="zab", tag="Z", bufs=3)
+        nc.tensor.transpose(zab[:], ab_rows[:], ident_b[:])
+        nc.scalar.copy(out=ab[:], in_=zab[:, 0:8])
+        permute_weights(0)
+        quant(0)
+        turn(1)
+        copy_out(1)
+        m1(0, 0)
+        m1(0, 1)
+        widen(6, "v")
+        quant(1)
+        act1(0)
+        turn(4)
+        copy_out(4)
+        m1(1, 0)
+        turn(2)
+        m1(1, 1)
+        permute_weights(1)
+        copy_out(2)
+        m2(0, 0)
+        m2(0, 1)
+        widen(7, "v")
+        quant(4)
+        quant(2)
+
+        TURNS = {-1: 3, 0: 5, 1: 6, 2: 7}
+        QUANTS = {0: 3, 1: 5, 2: 6, 3: 7}
+
+        def rows_of(p):
+            tp = token_pair(p)
+            return 2 * tp + 1, 2 * tp
+
+        turn(TURNS[-1])
+        for p in range(0, 8):
+            done = rows_of(p - 1) if p - 1 >= 4 else None
+            closing = rows_of(p - 2) if p - 2 >= 4 else None
+            if done:
+                zrow(done[0])
+            if p - 1 in TURNS:
+                copy_out(TURNS[p - 1])
+            if p in TURNS:
+                turn(TURNS[p])
+            if p + 2 < 8:
+                m1(p + 2, 0)
+            if p + 1 < 8:
+                act1(p + 1)
+            if done:
+                squares(done[0])
+            prod(p, 0)
+            if p + 1 < 8:
+                m2(p + 1, 0)
+            if p in QUANTS:
+                quant(QUANTS[p])
+            if p + 2 < 8:
+                m1(p + 2, 1)
+            if closing:
+                mask_and_sum(closing[0])
+            if done:
+                zrow(done[1])
+                squares(done[1])
+            prod(p, 1)
+            if p + 1 < 8:
+                m2(p + 1, 1)
+            if closing:
+                mask_and_sum(closing[1])
+            fquant(p)
+            if closing:
+                invert(token_pair(p - 2))
+                normalise(closing[0])
+                normalise(closing[1])
+        zrow(1)
+        squares(1)
+        zrow(0)
+        squares(0)
+        mask_and_sum(3)
+        mask_and_sum(2)
+        invert(1)
+        times_1024(1)
+        normalise(3, "s")
+        mask_and_sum(1)
+        mask_and_sum(0)
+        invert(0)
+        normalise(2, "s")
+        normalise(1)
+        normalise(0)

@@ -144,12 +144,14 @@ def tile_polysketchdegreefourcausalweights_d1p_kernel(
         def quant(p):
             nc.vector.quantize_mx(out=codes[p][:].bitcast(FP8X4), scales=scales[p][:], in_=grouped[p][:])
 
+        def permute_scales(g, engine):
+            engine.tensor_copy(
+                out=s_w[g][:].rearrange("p (t a r) -> p t a r", t=4, r=2), in_=s_raw[g][:].rearrange("p (a t r) -> p t a r", t=4, r=2)
+            )
+
         def permute_weights(g):
             nc.vector.tensor_copy(
                 out=w[g][:].rearrange("p (t a r) -> p t a r", t=4, r=8), in_=w_raw[g][:].rearrange("p (a t r) -> p t a r", t=4, r=8)
-            )
-            nc.vector.tensor_copy(
-                out=s_w[g][:].rearrange("p (t a r) -> p t a r", t=4, r=2), in_=s_raw[g][:].rearrange("p (a t r) -> p t a r", t=4, r=2)
             )
 
         def mx(out_ap, g, t, p, c0, c1):
@@ -186,9 +188,9 @@ def tile_polysketchdegreefourcausalweights_d1p_kernel(
 
         def prod(p, j):
             nc.vector.tensor_tensor(
-                out=feat[p][:, 512 * j : 512 * (j + 1)].rearrange("p (n t) -> p n t", t=4),
-                in0=state["m2", p, j][:].rearrange("p (t n) -> p n t", t=4),
-                in1=s1[p][:, :, P * j : P * (j + 1)].rearrange("p t n -> p n t"),
+                out=feat[p][:, 512 * j : 512 * (j + 1)].rearrange("p (c i t) -> p c t i", i=2, t=4),
+                in0=state["m2", p, j][:].rearrange("p (t c i) -> p c t i", t=4, i=2),
+                in1=s1[p][:, :, P * j : P * (j + 1)].rearrange("p t (c i) -> p c t i", i=2),
                 op=ALU.mult,
             )
 
@@ -277,6 +279,7 @@ def tile_polysketchdegreefourcausalweights_d1p_kernel(
         nc.tensor.transpose(zab[:], ab_rows[:], ident_b[:])
         nc.scalar.copy(out=ab[:], in_=zab[:, 0:8])
         permute_weights(0)
+        permute_scales(0, nc.vector)
         quant(0)
         turn(1)
         copy_out(1)
@@ -291,6 +294,7 @@ def tile_polysketchdegreefourcausalweights_d1p_kernel(
         turn(2)
         m1(1, 1)
         permute_weights(1)
+        permute_scales(1, nc.gpsimd)
         copy_out(2)
         m2(0, 0)
         m2(0, 1)

@@ -15,6 +15,9 @@ FP8X4 = mybir.dt.float8_e4m3fn_x4
 ALU = mybir.AluOpType
 ACT = mybir.ActivationFunctionType
 
+GROUPS = [("k", (0,)), ("k", (1,)), ("k", (2, 3)), ("q", (2, 3)), ("q", (0, 1))]
+ORDER = [("k", 0), ("k", 1), ("k", 2), ("k", 3), ("q", 3), ("q", 2), ("q", 1), ("q", 0)]
+
 FLOPS = 4 * 2 * S * D * R + 2 * R * (S * (S + 1) // 2)
 
 
@@ -22,7 +25,7 @@ def tile_polysketchdegreefourcausalweights_d1p_kernel(
     tc, q_bytes, q_scale, k, g1_words, g1_scales, g2_words, g2_scales, a, b, out
 ):
     nc = tc.nc
-    with tc.tile_pool(name="keep", bufs=1) as keep, tc.psum_pool(name="banks", bufs=2) as psum, tc.manual_schedule():
+    with tc.tile_pool(name="keep", bufs=1) as keep, tc.psum_pool(name="banks", bufs=2) as psum:
 
         def sb(name, shape, dtype):
             return keep.tile(shape, dtype, name=name, align_bytes=64)
@@ -40,15 +43,16 @@ def tile_polysketchdegreefourcausalweights_d1p_kernel(
         s_w = [sb("s_w1", [P, P], I32), sb("s_w2", [P, P], I32)]
         w_raw = [sb("w_raw1", [P, R], I32), sb("w_raw2", [P, R], I32)]
         w = [sb("w1", [P, R], I32), sb("w2", [P, R], I32)]
-        k_raw = [sb("k_raw%d" % i, [P, 2, D], BF16) for i in range(4)]
-        q_codes8 = [sb("q_lo", [P, 4, D], U8), sb("q_hi", [P, 4, D], U8)]
-        qs = sb("qs", [P, 8, 4], F32)
-        q_bf = [sb("q_bf%d" % i, [P, 2, D], BF16) for i in range(4)]
-        grouped = [sb("grouped%d" % i, [P, 4 * PAIR], BF16) for i in range(8)]
-        codes = [sb("codes%d" % i, [P, PAIR], U32) for i in range(8)]
-        scales = [sb("scales%d" % i, [P, PAIR], U8) for i in range(8)]
-        s1 = [sb("s1_%d" % i, [P, 4, PAIR], F32) for i in range(8)]
-        feat = [sb("feat%d" % i, [P, 4 * PAIR], BF16) for i in range(8)]
+        k_raw = [sb("k_raw%d" % i, [P, 2 * D], BF16) for i in range(4)]
+        q_codes8 = [sb("q_raw%d" % i, [P, 2 * D], U8) for i in range(4)]
+        qs = sb("qs", [P, 4, 8], F32)
+        q_bf = [sb("q_bf%d" % i, [P, 2 * D], BF16) for i in range(4)]
+        widths = [PAIR * len(g[1]) for g in GROUPS]
+        grouped = [sb("grouped%d" % i, [P, 4 * n], BF16) for i, n in enumerate(widths)]
+        codes = [sb("codes%d" % i, [P, n], U32) for i, n in enumerate(widths)]
+        scales = [sb("scales%d" % i, [P, n], U8) for i, n in enumerate(widths)]
+        s1 = [sb("s1_%d" % i, [P, 4, n], F32) for i, n in enumerate(widths)]
+        feat = {pair: sb("feat_%s%d" % pair, [P, 4 * PAIR], BF16) for pair in ORDER}
         fk_codes = sb("fk_codes", [P, S], U32)
         fk_scales = sb("fk_scales", [P, S], U8)
         fq_codes = [sb("fq_codes%d" % i, [P, PAIR], U32) for i in range(4)]
@@ -63,8 +67,8 @@ def tile_polysketchdegreefourcausalweights_d1p_kernel(
         make_identity(nc, ident[:])
         nc.scalar.copy(out=ident_b[:], in_=ident[:])
 
-        k_view = k[0].rearrange("(i p) d -> p i d", p=P)
-        q_view = q_bytes[0].rearrange("(i p) d -> p i d", p=P)
+        k_view = k[0].rearrange("(i p j) d -> p i (j d)", p=P, j=2)
+        q_view = q_bytes[0].rearrange("(i p j) d -> p i (j d)", p=P, j=2)
 
         def load_scale_rows(queue, g, src):
             view = src[0].bitcast(I32).rearrange("(q s) n -> s q n", s=4)
@@ -76,73 +80,65 @@ def tile_polysketchdegreefourcausalweights_d1p_kernel(
 
         nc.gpsimd.dma_start(out=ab_rows[0:4, :].rearrange("t (a r) -> t a r", r=8), in_=b.rearrange("(a t r) -> t a r", t=4, r=8))
         nc.gpsimd.dma_start(out=ab_rows[4:8, :].rearrange("t (a r) -> t a r", r=8), in_=a.rearrange("(a t r) -> t a r", t=4, r=8))
-        load_scale_rows(nc.sync, 0, g1_scales)
-        nc.sync.dma_start(out=qs[:], in_=q_scale[0].rearrange("(i p) j -> p i j", p=P))
-        nc.sync.dma_start(out=q_codes8[1][:], in_=q_view[:, 4:8, :])
-        nc.sync.dma_start(out=k_raw[0][:], in_=k_view[:, 0:2, :])
+        def load_q(tp):
+            nc.sync.dma_start(out=q_codes8[tp][:], in_=q_view[:, tp, :])
+
+        def load_k(tp):
+            nc.sync.dma_start(out=k_raw[tp][:], in_=k_view[:, tp, :])
+
+        nc.sync.dma_start(out=qs[:], in_=q_scale[0].rearrange("(i p j) b -> p i (j b)", p=P, j=2))
+        load_q(3)
+        load_k(0)
         load_words(0, g1_words)
-        nc.sync.dma_start(out=k_raw[1][:], in_=k_view[:, 2:4, :])
-        nc.sync.dma_start(out=q_codes8[0][:], in_=q_view[:, 0:4, :])
+        load_scale_rows(nc.sync, 0, g1_scales)
+        load_q(2)
+        load_k(1)
         load_words(1, g2_words)
-        nc.sync.dma_start(out=k_raw[2][:], in_=k_view[:, 4:6, :])
-        nc.sync.dma_start(out=k_raw[3][:], in_=k_view[:, 6:8, :])
+        load_q(1)
+        load_k(2)
         load_scale_rows(nc.sync, 1, g2_scales)
+        load_q(0)
+        load_k(3)
 
-        nc.gpsimd.memset(zeros[:], 0.0)
-        for i in range(7):
-            wid = P * (i + 1)
-            nc.sync.dma_start(out=out[0, P * i : P * (i + 1), wid:S], in_=zeros[:, 0 : S - wid])
-        nc.gpsimd.memset(mask[:], 1.0)
-        nc.gpsimd.affine_select(
-            out=mask[:, 0:P], in_=mask[:, 0:P], pattern=[[-1, P]], compare_op=ALU.is_ge, fill=0.0, base=0, channel_multiplier=1
-        )
-        for i in range(8):
-            nc.gpsimd.memset(rows[i][:, P * (i + 1) : P * (i + 1) + 1], 1024.0 * 512.0)
 
-        def k_words(pair):
-            return k_raw[pair][:].rearrange("p i d -> p (i d)").bitcast(F32)
-
-        Q_PAIRS = [3, 2, 1, 0]
+        place = {}
+        for g, (kind, pairs) in enumerate(GROUPS):
+            for n, tp in enumerate(pairs):
+                place[kind, tp] = (g, PAIR * n)
         state = {}
 
-        def is_q(p):
-            return p >= 4
-
-        def token_pair(p):
-            return Q_PAIRS[p - 4] if is_q(p) else p
-
-        def widen(p, engine, first=0, last=8):
-            tp = token_pair(p)
+        def widen(tp, engine, first=0, last=8):
             for n in range(first, last):
-                if True:
-                    j, blk = n // 4, n % 4
-                    i = 2 * tp + j
-                    src = q_codes8[i // 4][:, i % 4, P * blk : P * (blk + 1)].bitcast(FP8)
-                    dst = q_bf[tp][:, j, P * blk : P * (blk + 1)]
-                    sc = qs[:, i, blk : blk + 1]
-                    if engine == "v":
-                        nc.vector.tensor_scalar(out=dst, in0=src, scalar1=sc, scalar2=None, op0=ALU.mult)
-                    else:
-                        nc.scalar.activation(out=dst, in_=src, func=ACT.Copy, scale=sc)
+                cols = slice(P * n, P * (n + 1))
+                src = q_codes8[tp][:, cols].bitcast(FP8)
+                dst = q_bf[tp][:, cols]
+                sc = qs[:, tp, n : n + 1]
+                if engine == "v":
+                    nc.vector.tensor_scalar(out=dst, in0=src, scalar1=sc, scalar2=None, op0=ALU.mult)
+                else:
+                    nc.scalar.activation(out=dst, in_=src, func=ACT.Copy, scale=sc)
 
-        def turn(p):
-            words = q_bf[token_pair(p)][:].rearrange("p i d -> p (i d)").bitcast(F32) if is_q(p) else k_words(p)
-            z = bank("turn%d" % p, "Z", 3)
+        def turn(kind, tp):
+            words = (q_bf if kind == "q" else k_raw)[tp][:].bitcast(F32)
+            z = bank("turn_%s%d" % (kind, tp), "Z", 3)
             for j in range(2):
                 for u in range(2):
                     nc.tensor.transpose(
                         z[:, PAIR * u + P * j : PAIR * u + P * (j + 1)], words[:, 256 * j + u : 256 * (j + 1) : 2], ident[:]
                     )
-            state["turn", p] = z
+            state["turn", kind, tp] = z
 
-        def copy_out(p):
-            z = state["turn", p]
-            nc.scalar.copy(
-                out=grouped[p][:].bitcast(F32).rearrange("p (c u) -> p c u", u=2), in_=z[:].rearrange("p (u c) -> p c u", u=2)
-            )
+        def copy_out(kind, tp, engine="s"):
+            g, c0 = place[kind, tp]
+            dst = grouped[g][:, 4 * c0 : 4 * (c0 + PAIR)].bitcast(F32).rearrange("p (c j u) -> p c j u", j=2, u=2)
+            src = state["turn", kind, tp][:].rearrange("p (u j c) -> p c j u", u=2, j=2)
+            if engine == "s":
+                nc.scalar.copy(out=dst, in_=src)
+            else:
+                nc.vector.tensor_copy(out=dst, in_=src)
 
-        def quant(p):
-            nc.vector.quantize_mx(out=codes[p][:].bitcast(FP8X4), scales=scales[p][:], in_=grouped[p][:])
+        def quant(g):
+            nc.vector.quantize_mx(out=codes[g][:].bitcast(FP8X4), scales=scales[g][:], in_=grouped[g][:])
 
         def permute_scales(g, engine):
             engine.tensor_copy(
@@ -154,53 +150,69 @@ def tile_polysketchdegreefourcausalweights_d1p_kernel(
                 out=w[g][:].rearrange("p (t a r) -> p t a r", t=4, r=8), in_=w_raw[g][:].rearrange("p (a t r) -> p t a r", t=4, r=8)
             )
 
-        def mx(out_ap, g, t, p, c0, c1):
+        def mx(out_ap, weight, t, g, c0, c1):
             nc.tensor.matmul_mx(
                 out=out_ap,
-                lhsT=w[g][:, P * t : P * (t + 1)].bitcast(FP8X4),
-                lhsT_scale=s_w[g][:].bitcast(U8)[:, P * t : P * (t + 1)],
-                rhs=codes[p][:, c0:c1].bitcast(FP8X4),
-                rhs_scale=scales[p][:, c0:c1],
+                lhsT=w[weight][:, P * t : P * (t + 1)].bitcast(FP8X4),
+                lhsT_scale=s_w[weight][:].bitcast(U8)[:, P * t : P * (t + 1)],
+                rhs=codes[g][:, c0:c1].bitcast(FP8X4),
+                rhs_scale=scales[g][:, c0:c1],
                 start=True,
                 stop=True,
             )
 
-        def m1(p, h):
-            z = bank("m1_%d_%d" % (p, h), "A", 3)
-            for e in range(2):
-                mx(z[:, PAIR * e : PAIR * (e + 1)], 0, 2 * h + e, p, 0, PAIR)
-            state["m1", p, h] = z
+        units = []
+        for g, n in enumerate(widths):
+            step = 512 // n
+            for t in range(0, 4, step):
+                units.append((g, range(t, t + step)))
 
-        def act1(p):
-            base = 4 if is_q(p) else 0
-            for t in range(4):
-                z = state["m1", p, t // 2]
-                e = t % 2
+        def m1(i):
+            if i >= len(units):
+                return
+            g, ts = units[i]
+            z = bank("m1_%d" % i, "A", 3)
+            n = widths[g]
+            for e, t in enumerate(ts):
+                mx(z[:, n * e : n * (e + 1)], 0, t, g, 0, n)
+            state["m1", i] = z
+
+        def act1(i):
+            g, ts = units[i]
+            base = 4 if GROUPS[g][0] == "q" else 0
+            n = widths[g]
+            for e, t in enumerate(ts):
                 nc.scalar.activation(
-                    out=s1[p][:, t, :], in_=z[:, PAIR * e : PAIR * (e + 1)], func=ACT.Copy, scale=ab[:, base + t : base + t + 1]
+                    out=s1[g][:, t, :], in_=state["m1", i][:, n * e : n * (e + 1)], func=ACT.Copy, scale=ab[:, base + t : base + t + 1]
                 )
 
         def m2(p, j):
+            if p >= 8:
+                return
+            g, c0 = place[ORDER[p]]
             z = bank("m2_%d_%d" % (p, j), "B", 2)
             for t in range(4):
-                mx(z[:, P * t : P * (t + 1)], 1, t, p, P * j, P * (j + 1))
+                mx(z[:, P * t : P * (t + 1)], 1, t, g, c0 + P * j, c0 + P * (j + 1))
             state["m2", p, j] = z
 
         def prod(p, j):
+            g, c0 = place[ORDER[p]]
             nc.vector.tensor_tensor(
-                out=feat[p][:, 512 * j : 512 * (j + 1)].rearrange("p (c i t) -> p c t i", i=2, t=4),
+                out=feat[ORDER[p]][:, 512 * j : 512 * (j + 1)].rearrange("p (c i t) -> p c t i", i=2, t=4),
                 in0=state["m2", p, j][:].rearrange("p (t c i) -> p c t i", t=4, i=2),
-                in1=s1[p][:, :, P * j : P * (j + 1)].rearrange("p t (c i) -> p c t i", i=2),
+                in1=s1[g][:, :, c0 + P * j : c0 + P * (j + 1)].rearrange("p t (c i) -> p c t i", i=2),
                 op=ALU.mult,
             )
 
-        def fquant(p):
-            tp = token_pair(p)
-            if is_q(p):
-                nc.vector.quantize_mx(out=fq_codes[tp][:].bitcast(FP8X4), scales=fq_scales[tp][:], in_=feat[p][:])
+        def fquant(p, first=0, last=2):
+            kind, tp = ORDER[p]
+            src = feat[ORDER[p]][:, 512 * first : 512 * last]
+            if kind == "q":
+                cols = slice(P * first, P * last)
+                nc.vector.quantize_mx(out=fq_codes[tp][:, cols].bitcast(FP8X4), scales=fq_scales[tp][:, cols], in_=src)
             else:
-                cols = slice(PAIR * tp, PAIR * (tp + 1))
-                nc.vector.quantize_mx(out=fk_codes[:, cols].bitcast(FP8X4), scales=fk_scales[:, cols], in_=feat[p][:])
+                cols = slice(PAIR * tp + P * first, PAIR * tp + P * last)
+                nc.vector.quantize_mx(out=fk_codes[:, cols].bitcast(FP8X4), scales=fk_scales[:, cols], in_=src)
 
         def zrow(i):
             tp, j = i // 2, i % 2
@@ -254,12 +266,12 @@ def tile_polysketchdegreefourcausalweights_d1p_kernel(
         def invert(tp):
             nc.vector.reciprocal(out=rec[:, 2 * tp : 2 * tp + 2], in_=den[:, 2 * tp : 2 * tp + 2])
 
-        def normalise(i, engine="v"):
+        def normalise(i, engine="v", factor=True):
             width = P * (i + 1)
             row = rows[i]
             if engine == "v":
                 nc.vector.tensor_scalar(
-                    out=row[:, 0:width], in0=row[:, 0:width], scalar1=rec[:, i : i + 1], scalar2=1024.0, op0=ALU.mult, op1=ALU.mult
+                    out=row[:, 0:width], in0=row[:, 0:width], scalar1=rec[:, i : i + 1], scalar2=1024.0 if factor else 1.0, op0=ALU.mult, op1=ALU.mult
                 )
             else:
                 nc.scalar.activation(out=row[:, 0:width], in_=row[:, 0:width], func=ACT.Copy, scale=rec[:, i : i + 1])
@@ -270,95 +282,109 @@ def tile_polysketchdegreefourcausalweights_d1p_kernel(
                 out=rec[:, 2 * tp : 2 * tp + 2], in0=rec[:, 2 * tp : 2 * tp + 2], scalar1=1024.0, scalar2=None, op0=ALU.mult
             )
 
-        turn(0)
-        widen(4, "v")
-        widen(5, "s", 0, 6)
-        copy_out(0)
-        widen(5, "s", 6, 8)
+        def rows_of(p):
+            if p < 0 or ORDER[p][0] == "k":
+                return None
+            tp = ORDER[p][1]
+            return 2 * tp + 1, 2 * tp
+
+        turn("k", 0)
+        widen(3, "v")
+        copy_out("k", 0)
         zab = psum.tile([P, P], BF16, name="zab", tag="Z", bufs=3)
         nc.tensor.transpose(zab[:], ab_rows[:], ident_b[:])
         nc.scalar.copy(out=ab[:], in_=zab[:, 0:8])
+        quant(0)
         permute_weights(0)
         permute_scales(0, nc.vector)
-        quant(0)
-        turn(1)
-        copy_out(1)
-        m1(0, 0)
-        m1(0, 1)
-        widen(6, "v")
-        quant(1)
+        turn("k", 1)
+        copy_out("k", 1)
+        m1(0)
+        m1(1)
+        widen(2, "v")
         act1(0)
-        turn(4)
-        copy_out(4)
-        m1(1, 0)
-        turn(2)
-        m1(1, 1)
+        quant(1)
+        act1(1)
+        m1(2)
         permute_weights(1)
         permute_scales(1, nc.gpsimd)
-        copy_out(2)
+        nc.gpsimd.memset(zeros[:], 0.0)
+        for i in range(7):
+            wid = P * (i + 1)
+            nc.sync.dma_start(out=out[0, P * i : P * (i + 1), wid:S], in_=zeros[:, 0 : S - wid])
+        nc.gpsimd.memset(mask[:], 1.0)
+        nc.gpsimd.affine_select(
+            out=mask[:, 0:P], in_=mask[:, 0:P], pattern=[[-1, P]], compare_op=ALU.is_ge, fill=0.0, base=0, channel_multiplier=1
+        )
+        for i in range(8):
+            nc.gpsimd.memset(rows[i][:, P * (i + 1) : P * (i + 1) + 1], 1024.0 * 512.0)
+        m1(3)
         m2(0, 0)
         m2(0, 1)
-        widen(7, "v")
-        quant(4)
+        turn("k", 2)
+        copy_out("k", 2)
+        turn("k", 3)
+        copy_out("k", 3, "v")
+        act1(2)
+        act1(3)
         quant(2)
-
-        TURNS = {-1: 3, 0: 5, 1: 6, 2: 7}
-        QUANTS = {0: 3, 1: 5, 2: 6, 3: 7}
-
-        def rows_of(p):
-            tp = token_pair(p)
-            return 2 * tp + 1, 2 * tp
-
-        turn(TURNS[-1])
-        for p in range(0, 8):
-            done = rows_of(p - 1) if p - 1 >= 4 else None
-            closing = rows_of(p - 2) if p - 2 >= 4 else None
-            if done:
-                zrow(done[0])
-            if p - 1 in TURNS:
-                copy_out(TURNS[p - 1])
-            if p in TURNS:
-                turn(TURNS[p])
-            if p + 2 < 8:
-                m1(p + 2, 0)
-            if p + 1 < 8:
-                act1(p + 1)
-            if done:
-                squares(done[0])
-            prod(p, 0)
-            if p + 1 < 8:
-                m2(p + 1, 0)
-            if p in QUANTS:
-                quant(QUANTS[p])
-            if p + 2 < 8:
-                m1(p + 2, 1)
+        m1(4)
+        m1(5)
+        widen(1, "v")
+        turn("q", 3)
+        copy_out("q", 3)
+        turn("q", 2)
+        copy_out("q", 2)
+        quant(3)
+        widen(0, "v")
+        UNITS = {0: [4, 5], 1: [6, 7], 2: [8, 9], 3: [10, 11], 4: [12, 13], 5: [14, 15], 6: [], 7: []}
+        for p in range(8):
+            done = rows_of(p - 1)
+            closing = rows_of(p - 2)
+            if p == 1:
+                turn("q", 1)
+                copy_out("q", 1)
+                turn("q", 0)
+                copy_out("q", 0)
+                quant(4)
             if closing:
                 mask_and_sum(closing[0])
+            prod(p, 0)
+            m2(p + 1, 0)
+            if closing:
+                mask_and_sum(closing[1])
+            if p:
+                fquant(p - 1)
+            for i in UNITS[p]:
+                act1(i)
+                m1(i + 2)
+            if done:
+                zrow(done[0])
+                squares(done[0])
+            if closing:
+                invert(closing[1] // 2)
+            prod(p, 1)
+            m2(p + 1, 1)
             if done:
                 zrow(done[1])
                 squares(done[1])
-            prod(p, 1)
-            if p + 1 < 8:
-                m2(p + 1, 1)
             if closing:
-                mask_and_sum(closing[1])
-            fquant(p)
-            if closing:
-                invert(token_pair(p - 2))
                 normalise(closing[0])
                 normalise(closing[1])
+        fquant(7, 1, 2)
         zrow(1)
         squares(1)
+        fquant(7, 0, 1)
         zrow(0)
         squares(0)
         mask_and_sum(3)
         mask_and_sum(2)
         invert(1)
-        times_1024(1)
-        normalise(3, "s")
         mask_and_sum(1)
+        times_1024(1)
         mask_and_sum(0)
+        normalise(3, "s")
         invert(0)
-        normalise(2, "s")
+        normalise(2, factor=False)
         normalise(1)
         normalise(0)

@@ -25,7 +25,7 @@ def tile_polysketchdegreefourcausalweights_d1p_kernel(
     tc, q_bytes, q_scale, k, g1_words, g1_scales, g2_words, g2_scales, a, b, out
 ):
     nc = tc.nc
-    with tc.tile_pool(name="keep", bufs=1) as keep, tc.psum_pool(name="banks", bufs=2) as psum:
+    with tc.tile_pool(name="keep", bufs=1) as keep, tc.psum_pool(name="banks", bufs=2) as psum, tc.manual_schedule(engines={mybir.EngineType.SP}):
 
         def sb(name, shape, dtype):
             return keep.tile(shape, dtype, name=name, align_bytes=64)
@@ -64,6 +64,10 @@ def tile_polysketchdegreefourcausalweights_d1p_kernel(
         nc.vector.memset(s_raw[0][:], 0)
         nc.vector.memset(ab_rows[:], 0.0)
         nc.vector.memset(s_raw[1][:], 0)
+        nc.vector.memset(mask[:], 1.0)
+        nc.vector.memset(zeros[:], 0.0)
+        for i in range(8):
+            nc.vector.memset(rows[i][:, P * (i + 1) : P * (i + 1) + 1], 1024.0 * 512.0)
         make_identity(nc, ident[:])
         nc.scalar.copy(out=ident_b[:], in_=ident[:])
 
@@ -80,6 +84,10 @@ def tile_polysketchdegreefourcausalweights_d1p_kernel(
 
         nc.gpsimd.dma_start(out=ab_rows[0:4, :].rearrange("t (a r) -> t a r", r=8), in_=b.rearrange("(a t r) -> t a r", t=4, r=8))
         nc.gpsimd.dma_start(out=ab_rows[4:8, :].rearrange("t (a r) -> t a r", r=8), in_=a.rearrange("(a t r) -> t a r", t=4, r=8))
+        nc.gpsimd.affine_select(
+            out=mask[:, 0:P], in_=mask[:, 0:P], pattern=[[-1, P]], compare_op=ALU.is_ge, fill=0.0, base=0, channel_multiplier=1
+        )
+
         def load_q(tp):
             nc.sync.dma_start(out=q_codes8[tp][:], in_=q_view[:, tp, :])
 
@@ -198,9 +206,9 @@ def tile_polysketchdegreefourcausalweights_d1p_kernel(
         def prod(p, j):
             g, c0 = place[ORDER[p]]
             nc.vector.tensor_tensor(
-                out=feat[ORDER[p]][:, 512 * j : 512 * (j + 1)].rearrange("p (c i t) -> p c t i", i=2, t=4),
-                in0=state["m2", p, j][:].rearrange("p (t c i) -> p c t i", t=4, i=2),
-                in1=s1[g][:, :, c0 + P * j : c0 + P * (j + 1)].rearrange("p t (c i) -> p c t i", i=2),
+                out=feat[ORDER[p]][:, 512 * j : 512 * (j + 1)].rearrange("p (c i t) -> p c t i", i=4, t=4),
+                in0=state["m2", p, j][:].rearrange("p (t c i) -> p c t i", t=4, i=4),
+                in1=s1[g][:, :, c0 + P * j : c0 + P * (j + 1)].rearrange("p t (c i) -> p c t i", i=4),
                 op=ALU.mult,
             )
 
@@ -308,16 +316,9 @@ def tile_polysketchdegreefourcausalweights_d1p_kernel(
         m1(2)
         permute_weights(1)
         permute_scales(1, nc.gpsimd)
-        nc.gpsimd.memset(zeros[:], 0.0)
         for i in range(7):
             wid = P * (i + 1)
             nc.sync.dma_start(out=out[0, P * i : P * (i + 1), wid:S], in_=zeros[:, 0 : S - wid])
-        nc.gpsimd.memset(mask[:], 1.0)
-        nc.gpsimd.affine_select(
-            out=mask[:, 0:P], in_=mask[:, 0:P], pattern=[[-1, P]], compare_op=ALU.is_ge, fill=0.0, base=0, channel_multiplier=1
-        )
-        for i in range(8):
-            nc.gpsimd.memset(rows[i][:, P * (i + 1) : P * (i + 1) + 1], 1024.0 * 512.0)
         m1(3)
         m2(0, 0)
         m2(0, 1)

@@ -3,7 +3,10 @@ from concourse.masks import make_identity
 
 S, D, R = 1024, 512, 512
 P = 128
-PAIR = 256
+PAIR = 2 * P
+BANK = 512
+PACK = 4
+RUN = 8
 
 F32 = mybir.dt.float32
 BF16 = mybir.dt.bfloat16
@@ -17,6 +20,7 @@ ACT = mybir.ActivationFunctionType
 
 GROUPS = [("k", (0,)), ("k", (1,)), ("k", (2, 3)), ("q", (2, 3)), ("q", (0, 1))]
 ORDER = [("k", 0), ("k", 1), ("k", 2), ("k", 3), ("q", 3), ("q", 2), ("q", 1), ("q", 0)]
+DIVIDED_ON_SCALAR = (4, 3)
 
 FLOPS = 4 * 2 * S * D * R + 2 * R * (S * (S + 1) // 2)
 
@@ -25,367 +29,427 @@ def tile_polysketchdegreefourcausalweights_d1p_kernel(
     tc, q_bytes, q_scale, k, g1_words, g1_scales, g2_words, g2_scales, a, b, out
 ):
     nc = tc.nc
-    with tc.tile_pool(name="keep", bufs=1) as keep, tc.psum_pool(name="banks", bufs=2) as psum, tc.manual_schedule(engines={mybir.EngineType.SP}):
+    with tc.tile_pool(name="keep", bufs=1) as keep, tc.psum_pool(name="banks", bufs=2) as psum, tc.manual_schedule():
 
         def sb(name, shape, dtype):
             return keep.tile(shape, dtype, name=name, align_bytes=64)
 
         def bank(name, tag, bufs):
-            return psum.tile([P, 512], F32, name=name, tag=tag, bufs=bufs)
+            return psum.tile([P, BANK], F32, name=name, tag=tag, bufs=bufs)
 
-        ident = sb("ident", [P, P], F32)
-        ident_b = sb("ident_b", [P, P], BF16)
-        mask = sb("mask", [P, P + 4], F32)
+        identity = sb("identity", [P, P], F32)
+        identity_bf = sb("identity_bf", [P, P], BF16)
+        mask = sb("mask", [P, P + 3], F32)
         zeros = sb("zeros", [P, S - P], F32)
-        ab_rows = sb("ab_rows", [P, P], BF16)
-        ab = sb("ab", [P, 8], F32)
-        s_raw = [sb("s_raw1", [P, P], I32), sb("s_raw2", [P, P], I32)]
-        s_w = [sb("s_w1", [P, P], I32), sb("s_w2", [P, P], I32)]
-        w_raw = [sb("w_raw1", [P, R], I32), sb("w_raw2", [P, R], I32)]
-        w = [sb("w1", [P, R], I32), sb("w2", [P, R], I32)]
+        factor_rows = sb("factor_rows", [P, P], BF16)
+        factors = sb("factors", [P, 2 * PACK], F32)
+        scale_rows = [sb("scale_rows%d" % i, [P, P], I32) for i in range(2)]
+        words = [sb("words%d" % i, [P, R], I32) for i in range(2)]
+        w_scales = [sb("w_scales%d" % i, [P, P], I32) for i in range(2)]
+        w_codes = [sb("w_codes%d" % i, [P, R], I32) for i in range(2)]
         k_raw = [sb("k_raw%d" % i, [P, 2 * D], BF16) for i in range(4)]
-        q_codes8 = [sb("q_raw%d" % i, [P, 2 * D], U8) for i in range(4)]
-        qs = sb("qs", [P, 4, 8], F32)
+        q_raw = [sb("q_raw%d" % i, [P, 2, 2 * D], U8) for i in range(2)]
+        q_scales = sb("q_scales", [P, 4, 8], F32)
         q_bf = [sb("q_bf%d" % i, [P, 2 * D], BF16) for i in range(4)]
-        widths = [PAIR * len(g[1]) for g in GROUPS]
-        grouped = [sb("grouped%d" % i, [P, 4 * n], BF16) for i, n in enumerate(widths)]
+        widths = [PAIR * len(pairs) for kind, pairs in GROUPS]
+        grouped = [sb("grouped%d" % i, [P, PACK * n], BF16) for i, n in enumerate(widths)]
         codes = [sb("codes%d" % i, [P, n], U32) for i, n in enumerate(widths)]
         scales = [sb("scales%d" % i, [P, n], U8) for i, n in enumerate(widths)]
-        s1 = [sb("s1_%d" % i, [P, 4, n], F32) for i, n in enumerate(widths)]
-        feat = {pair: sb("feat_%s%d" % pair, [P, 4 * PAIR], BF16) for pair in ORDER}
+        first = [sb("first%d" % i, [P, PACK, n], F32) for i, n in enumerate(widths)]
+        feature = {pair: sb("feature_%s%d" % pair, [P, PACK * PAIR], BF16) for pair in ORDER}
         fk_codes = sb("fk_codes", [P, S], U32)
         fk_scales = sb("fk_scales", [P, S], U8)
         fq_codes = [sb("fq_codes%d" % i, [P, PAIR], U32) for i in range(4)]
         fq_scales = [sb("fq_scales%d" % i, [P, PAIR], U8) for i in range(4)]
-        rows = [sb("row%d" % i, [P, P * (i + 1) + 4], F32) for i in range(8)]
-        den = sb("den", [P, 8], F32)
-        rec = sb("rec", [P, 8], F32)
+        rows = [sb("rows%d" % r, [P, P * (r + 1) + 3], F32) for r in range(8)]
+        total = sb("total", [P, 8], F32)
+        inverse = sb("inverse", [P, 8], F32)
 
-        nc.vector.memset(s_raw[0][:], 0)
-        nc.vector.memset(ab_rows[:], 0.0)
-        nc.vector.memset(s_raw[1][:], 0)
+        nc.vector.memset(scale_rows[0][:], 0)
+        nc.vector.memset(factor_rows[:], 0.0)
+        nc.vector.memset(scale_rows[1][:], 0)
         nc.vector.memset(mask[:], 1.0)
         nc.vector.memset(zeros[:], 0.0)
-        for i in range(8):
-            nc.vector.memset(rows[i][:, P * (i + 1) : P * (i + 1) + 1], 1024.0 * 512.0)
-        make_identity(nc, ident[:])
-        nc.scalar.copy(out=ident_b[:], in_=ident[:])
+        for r in range(8):
+            nc.vector.memset(rows[r][:, P * (r + 1) : P * (r + 1) + 1], 512.0 * 1024.0)
+        make_identity(nc, identity[:])
 
         k_view = k[0].rearrange("(i p j) d -> p i (j d)", p=P, j=2)
         q_view = q_bytes[0].rearrange("(i p j) d -> p i (j d)", p=P, j=2)
 
-        def load_scale_rows(queue, g, src):
+        def load_scale_rows(i, src):
             view = src[0].bitcast(I32).rearrange("(q s) n -> s q n", s=4)
             for s in range(4):
-                queue.dma_start(out=s_raw[g][s : P : 32, :], in_=view[s])
+                nc.sync.dma_start(out=scale_rows[i][s : P : 32, :], in_=view[s])
 
-        def load_words(g, src):
-            nc.sync.dma_start(out=w_raw[g][:], in_=src[0].rearrange("p n t -> p (n t)").bitcast(I32))
+        def load_words(i, src):
+            nc.sync.dma_start(out=words[i][:], in_=src[0].rearrange("p n t -> p (n t)").bitcast(I32))
 
-        nc.gpsimd.dma_start(out=ab_rows[0:4, :].rearrange("t (a r) -> t a r", r=8), in_=b.rearrange("(a t r) -> t a r", t=4, r=8))
-        nc.gpsimd.dma_start(out=ab_rows[4:8, :].rearrange("t (a r) -> t a r", r=8), in_=a.rearrange("(a t r) -> t a r", t=4, r=8))
+        def load_factor(row, src):
+            nc.gpsimd.dma_start(
+                out=factor_rows[row : row + PACK, :].rearrange("t (c r) -> t c r", r=RUN),
+                in_=src.rearrange("(c t r) -> t c r", t=PACK, r=RUN),
+            )
+
+        def load_q(half):
+            nc.sync.dma_start(out=q_raw[half][:], in_=q_view[:, 2 * half : 2 * half + 2, :])
+
+        def load_k(pair):
+            nc.sync.dma_start(out=k_raw[pair][:], in_=k_view[:, pair, :])
+
+        load_factor(0, b)
+        load_factor(PACK, a)
         nc.gpsimd.affine_select(
             out=mask[:, 0:P], in_=mask[:, 0:P], pattern=[[-1, P]], compare_op=ALU.is_ge, fill=0.0, base=0, channel_multiplier=1
         )
-
-        def load_q(tp):
-            nc.sync.dma_start(out=q_codes8[tp][:], in_=q_view[:, tp, :])
-
-        def load_k(tp):
-            nc.sync.dma_start(out=k_raw[tp][:], in_=k_view[:, tp, :])
-
-        nc.sync.dma_start(out=qs[:], in_=q_scale[0].rearrange("(i p j) b -> p i (j b)", p=P, j=2))
-        load_q(3)
+        nc.sync.dma_start(out=q_scales[:], in_=q_scale[0].rearrange("(i p j) c -> p i (j c)", p=P, j=2))
+        load_q(1)
         load_k(0)
         load_words(0, g1_words)
-        load_scale_rows(nc.sync, 0, g1_scales)
-        load_q(2)
+        load_scale_rows(0, g1_scales)
         load_k(1)
         load_words(1, g2_words)
-        load_q(1)
-        load_k(2)
-        load_scale_rows(nc.sync, 1, g2_scales)
         load_q(0)
+        load_k(2)
+        load_scale_rows(1, g2_scales)
         load_k(3)
+        for r in range(7):
+            width = P * (r + 1)
+            nc.sync.dma_start(out=out[0, P * r : P * (r + 1), width:S], in_=zeros[:, 0 : S - width])
 
+        nc.scalar.copy(out=identity_bf[:], in_=identity[:])
 
         place = {}
         for g, (kind, pairs) in enumerate(GROUPS):
-            for n, tp in enumerate(pairs):
-                place[kind, tp] = (g, PAIR * n)
-        state = {}
+            for n, pair in enumerate(pairs):
+                place[kind, pair] = (g, PAIR * n)
+        held = {}
 
-        def widen(tp, engine, first=0, last=8):
-            for n in range(first, last):
+        def turn_factors():
+            z = psum.tile([P, P], BF16, name="turned_factors", tag="Z", bufs=3)
+            nc.tensor.transpose(z[:], factor_rows[:], identity_bf[:])
+            nc.scalar.copy(out=factors[:], in_=z[:, 0 : 2 * PACK])
+
+        def permute_codes(i):
+            nc.vector.tensor_copy(
+                out=w_codes[i][:].rearrange("p (t c r) -> p t c r", t=PACK, r=RUN),
+                in_=words[i][:].rearrange("p (c t r) -> p t c r", t=PACK, r=RUN),
+            )
+
+        def permute_scales(i, engine):
+            engine.tensor_copy(
+                out=w_scales[i][:].rearrange("p (t c r) -> p t c r", t=PACK, r=RUN // 4),
+                in_=scale_rows[i][:].rearrange("p (c t r) -> p t c r", t=PACK, r=RUN // 4),
+            )
+
+        def widen(pair, blocks, engine):
+            for n in blocks:
                 cols = slice(P * n, P * (n + 1))
-                src = q_codes8[tp][:, cols].bitcast(FP8)
-                dst = q_bf[tp][:, cols]
-                sc = qs[:, tp, n : n + 1]
-                if engine == "v":
-                    nc.vector.tensor_scalar(out=dst, in0=src, scalar1=sc, scalar2=None, op0=ALU.mult)
+                src = q_raw[pair // 2][:, pair % 2, cols].bitcast(FP8)
+                dst = q_bf[pair][:, cols]
+                scale = q_scales[:, pair, n : n + 1]
+                if engine == "vector":
+                    nc.vector.tensor_scalar(out=dst, in0=src, scalar1=scale, scalar2=None, op0=ALU.mult)
                 else:
-                    nc.scalar.activation(out=dst, in_=src, func=ACT.Copy, scale=sc)
+                    nc.scalar.activation(out=dst, in_=src, func=ACT.Copy, scale=scale)
 
-        def turn(kind, tp):
-            words = (q_bf if kind == "q" else k_raw)[tp][:].bitcast(F32)
-            z = bank("turn_%s%d" % (kind, tp), "Z", 3)
+        def turn(kind, pair):
+            pairs_of_bf = (q_bf if kind == "q" else k_raw)[pair][:].bitcast(F32)
+            z = bank("turned_%s%d" % (kind, pair), "Z", 3)
             for j in range(2):
                 for u in range(2):
                     nc.tensor.transpose(
-                        z[:, PAIR * u + P * j : PAIR * u + P * (j + 1)], words[:, 256 * j + u : 256 * (j + 1) : 2], ident[:]
+                        z[:, PAIR * u + P * j : PAIR * u + P * (j + 1)],
+                        pairs_of_bf[:, PAIR * j + u : PAIR * (j + 1) : 2],
+                        identity[:],
                     )
-            state["turn", kind, tp] = z
+            held["turned", kind, pair] = z
 
-        def copy_out(kind, tp, engine="s"):
-            g, c0 = place[kind, tp]
-            dst = grouped[g][:, 4 * c0 : 4 * (c0 + PAIR)].bitcast(F32).rearrange("p (c j u) -> p c j u", j=2, u=2)
-            src = state["turn", kind, tp][:].rearrange("p (u j c) -> p c j u", u=2, j=2)
-            if engine == "s":
+        def copy_out(kind, pair, engine="scalar"):
+            g, c0 = place[kind, pair]
+            dst = grouped[g][:, PACK * c0 : PACK * (c0 + PAIR)].bitcast(F32).rearrange("p (c j u) -> p c j u", j=2, u=2)
+            src = held["turned", kind, pair][:].rearrange("p (u j c) -> p c j u", u=2, j=2)
+            if engine == "scalar":
                 nc.scalar.copy(out=dst, in_=src)
             else:
                 nc.vector.tensor_copy(out=dst, in_=src)
 
-        def quant(g):
+        def quantise(g):
             nc.vector.quantize_mx(out=codes[g][:].bitcast(FP8X4), scales=scales[g][:], in_=grouped[g][:])
 
-        def permute_scales(g, engine):
-            engine.tensor_copy(
-                out=s_w[g][:].rearrange("p (t a r) -> p t a r", t=4, r=2), in_=s_raw[g][:].rearrange("p (a t r) -> p t a r", t=4, r=2)
-            )
-
-        def permute_weights(g):
-            nc.vector.tensor_copy(
-                out=w[g][:].rearrange("p (t a r) -> p t a r", t=4, r=8), in_=w_raw[g][:].rearrange("p (a t r) -> p t a r", t=4, r=8)
-            )
-
-        def mx(out_ap, weight, t, g, c0, c1):
+        def project(dst, i, t, g, c0, c1):
             nc.tensor.matmul_mx(
-                out=out_ap,
-                lhsT=w[weight][:, P * t : P * (t + 1)].bitcast(FP8X4),
-                lhsT_scale=s_w[weight][:].bitcast(U8)[:, P * t : P * (t + 1)],
+                out=dst,
+                lhsT=w_codes[i][:, P * t : P * (t + 1)].bitcast(FP8X4),
+                lhsT_scale=w_scales[i][:].bitcast(U8)[:, P * t : P * (t + 1)],
                 rhs=codes[g][:, c0:c1].bitcast(FP8X4),
                 rhs_scale=scales[g][:, c0:c1],
                 start=True,
                 stop=True,
             )
 
-        units = []
+        first_banks = []
         for g, n in enumerate(widths):
-            step = 512 // n
-            for t in range(0, 4, step):
-                units.append((g, range(t, t + step)))
+            for t in range(0, PACK, BANK // n):
+                first_banks.append((g, t, BANK // n))
 
-        def m1(i):
-            if i >= len(units):
-                return
-            g, ts = units[i]
-            z = bank("m1_%d" % i, "A", 3)
-            n = widths[g]
-            for e, t in enumerate(ts):
-                mx(z[:, n * e : n * (e + 1)], 0, t, g, 0, n)
-            state["m1", i] = z
+        def project_first(n):
+            g, t0, count = first_banks[n]
+            z = bank("first_bank%d" % n, "A", 3)
+            for e in range(count):
+                project(z[:, widths[g] * e : widths[g] * (e + 1)], 0, t0 + e, g, 0, widths[g])
+            held["first", n] = z
 
-        def act1(i):
-            g, ts = units[i]
-            base = 4 if GROUPS[g][0] == "q" else 0
-            n = widths[g]
-            for e, t in enumerate(ts):
+        def scale_first(n):
+            g, t0, count = first_banks[n]
+            column = PACK if GROUPS[g][0] == "q" else 0
+            for e in range(count):
                 nc.scalar.activation(
-                    out=s1[g][:, t, :], in_=state["m1", i][:, n * e : n * (e + 1)], func=ACT.Copy, scale=ab[:, base + t : base + t + 1]
+                    out=first[g][:, t0 + e, :],
+                    in_=held["first", n][:, widths[g] * e : widths[g] * (e + 1)],
+                    func=ACT.Copy,
+                    scale=factors[:, column + t0 + e : column + t0 + e + 1],
                 )
 
-        def m2(p, j):
-            if p >= 8:
-                return
-            g, c0 = place[ORDER[p]]
-            z = bank("m2_%d_%d" % (p, j), "B", 2)
-            for t in range(4):
-                mx(z[:, P * t : P * (t + 1)], 1, t, g, c0 + P * j, c0 + P * (j + 1))
-            state["m2", p, j] = z
+        def project_second(n, half):
+            g, c0 = place[ORDER[n]]
+            z = bank("second_bank%d_%d" % (n, half), "B", 2)
+            for t in range(PACK):
+                project(z[:, P * t : P * (t + 1)], 1, t, g, c0 + P * half, c0 + P * (half + 1))
+            held["second", n, half] = z
 
-        def prod(p, j):
-            g, c0 = place[ORDER[p]]
+        def multiply(n, half):
+            g, c0 = place[ORDER[n]]
             nc.vector.tensor_tensor(
-                out=feat[ORDER[p]][:, 512 * j : 512 * (j + 1)].rearrange("p (c i t) -> p c t i", i=4, t=4),
-                in0=state["m2", p, j][:].rearrange("p (t c i) -> p c t i", t=4, i=4),
-                in1=s1[g][:, :, c0 + P * j : c0 + P * (j + 1)].rearrange("p t (c i) -> p c t i", i=4),
+                out=feature[ORDER[n]][:, BANK * half : BANK * (half + 1)].rearrange("p (c i t) -> p c t i", i=4, t=PACK),
+                in0=held["second", n, half][:].rearrange("p (t c i) -> p c t i", t=PACK, i=4),
+                in1=first[g][:, :, c0 + P * half : c0 + P * (half + 1)].rearrange("p t (c i) -> p c t i", i=4),
                 op=ALU.mult,
             )
 
-        def fquant(p, first=0, last=2):
-            kind, tp = ORDER[p]
-            src = feat[ORDER[p]][:, 512 * first : 512 * last]
+        def quantise_features(n, halves=(0, 1)):
+            kind, pair = ORDER[n]
+            c0, c1 = P * halves[0], P * (halves[-1] + 1)
+            src = feature[ORDER[n]][:, PACK * c0 : PACK * c1]
             if kind == "q":
-                cols = slice(P * first, P * last)
-                nc.vector.quantize_mx(out=fq_codes[tp][:, cols].bitcast(FP8X4), scales=fq_scales[tp][:, cols], in_=src)
+                dst, dst_scales = fq_codes[pair][:, c0:c1], fq_scales[pair][:, c0:c1]
             else:
-                cols = slice(PAIR * tp + P * first, PAIR * tp + P * last)
-                nc.vector.quantize_mx(out=fk_codes[:, cols].bitcast(FP8X4), scales=fk_scales[:, cols], in_=src)
+                cols = slice(PAIR * pair + c0, PAIR * pair + c1)
+                dst, dst_scales = fk_codes[:, cols], fk_scales[:, cols]
+            nc.vector.quantize_mx(out=dst.bitcast(FP8X4), scales=dst_scales, in_=src)
 
-        def zrow(i):
-            tp, j = i // 2, i % 2
-            width = P * (i + 1)
-            banks = []
-            for c0 in range(0, width, 512):
-                z = bank("z%d_%d" % (i, c0), "Z", 3)
-                left = min(512, width - c0)
-                x = 0
-                while x < left:
-                    n = 512 if left - x >= 512 else (256 if left - x >= 256 else 128)
-                    nc.tensor.matmul_mx(
-                        out=z[:, x : x + n],
-                        lhsT=fq_codes[tp][:, P * j : P * (j + 1)].bitcast(FP8X4),
-                        lhsT_scale=fq_scales[tp][:, P * j : P * (j + 1)],
-                        rhs=fk_codes[:, c0 + x : c0 + x + n].bitcast(FP8X4),
-                        rhs_scale=fk_scales[:, c0 + x : c0 + x + n],
-                        start=True,
-                        stop=True,
-                    )
-                    x += n
-                banks.append((c0, left, z))
-            state["z", i] = banks
+        parts = [(r, h) for r in range(7, -1, -1) for h in range((r + 4) // 4)]
 
-        def squares(i):
-            width = P * (i + 1)
-            row = rows[i]
-            n_acc = 0
-            for c0, left, z in state["z", i]:
-                off = min(left, width - P - c0)
-                if off > 0:
-                    nc.scalar.activation(
-                        out=row[:, c0 : c0 + off],
-                        in_=z[:, 0:off],
-                        func=ACT.Square,
-                        accum_out=row[:, width + 1 + n_acc : width + 2 + n_acc],
-                    )
-                    n_acc += 1
-                if off < left:
-                    nc.scalar.activation(out=row[:, width - P : width], in_=z[:, off:left], func=ACT.Square)
-            state["n_acc", i] = n_acc
-
-        def mask_and_sum(i):
-            width = P * (i + 1)
-            n = 1 + state["n_acc", i]
-            part = rows[i][:, width - P : width + n]
-            nc.vector.scalar_tensor_tensor(
-                out=part, in0=part, scalar=1.0, in1=mask[:, 0 : P + n], op0=ALU.mult, op1=ALU.mult, accum_out=den[:, i : i + 1]
-            )
-
-        def invert(tp):
-            nc.vector.reciprocal(out=rec[:, 2 * tp : 2 * tp + 2], in_=den[:, 2 * tp : 2 * tp + 2])
-
-        def normalise(i, engine="v", factor=True):
-            width = P * (i + 1)
-            row = rows[i]
-            if engine == "v":
-                nc.vector.tensor_scalar(
-                    out=row[:, 0:width], in0=row[:, 0:width], scalar1=rec[:, i : i + 1], scalar2=1024.0 if factor else 1.0, op0=ALU.mult, op1=ALU.mult
+        def product(n):
+            r, h = parts[n]
+            rows_of_pair = slice(P * (r % 2), P * (r % 2 + 1))
+            z = bank("z%d_%d" % (r, h), "Z", 3)
+            c0, end = BANK * h, min(P * (r + 1), BANK * (h + 1))
+            c = c0
+            while c < end:
+                step = max(m for m in (512, 256, 128) if c + m <= end)
+                nc.tensor.matmul_mx(
+                    out=z[:, c - c0 : c - c0 + step],
+                    lhsT=fq_codes[r // 2][:, rows_of_pair].bitcast(FP8X4),
+                    lhsT_scale=fq_scales[r // 2][:, rows_of_pair],
+                    rhs=fk_codes[:, c : c + step].bitcast(FP8X4),
+                    rhs_scale=fk_scales[:, c : c + step],
+                    start=True,
+                    stop=True,
                 )
-            else:
-                nc.scalar.activation(out=row[:, 0:width], in_=row[:, 0:width], func=ACT.Copy, scale=rec[:, i : i + 1])
-            nc.sync.dma_start(out=out[0, P * i : P * (i + 1), 0:width], in_=row[:, 0:width])
+                c += step
+            held["z", r, h] = z
 
-        def times_1024(tp):
-            nc.vector.tensor_scalar(
-                out=rec[:, 2 * tp : 2 * tp + 2], in0=rec[:, 2 * tp : 2 * tp + 2], scalar1=1024.0, scalar2=None, op0=ALU.mult
+        def square(n):
+            r, h = parts[n]
+            diagonal = P * r
+            c0, end = BANK * h, min(P * (r + 1), BANK * (h + 1))
+            left = min(end, diagonal)
+            if left > c0:
+                sums = P * (r + 1) + 1 + h
+                nc.scalar.activation(
+                    out=rows[r][:, c0:left], in_=held["z", r, h][:, 0 : left - c0], func=ACT.Square, accum_out=rows[r][:, sums : sums + 1]
+                )
+            if end > diagonal:
+                nc.scalar.activation(out=rows[r][:, diagonal:end], in_=held["z", r, h][:, diagonal - c0 : end - c0], func=ACT.Square)
+
+        def mask_and_sum(r):
+            part = rows[r][:, P * r : P * (r + 1) + 1 + (r + 3) // 4]
+            nc.vector.scalar_tensor_tensor(
+                out=part,
+                in0=part,
+                scalar=1.0,
+                in1=mask[:, 0 : P + 1 + (r + 3) // 4],
+                op0=ALU.mult,
+                op1=ALU.mult,
+                accum_out=total[:, r : r + 1],
             )
 
-        def rows_of(p):
-            if p < 0 or ORDER[p][0] == "k":
-                return None
-            tp = ORDER[p][1]
-            return 2 * tp + 1, 2 * tp
+        def holds_factor(pair):
+            return any(r // 2 == pair for r in DIVIDED_ON_SCALAR)
 
+        def invert(pair):
+            both = inverse[:, 2 * pair : 2 * pair + 2]
+            nc.vector.reciprocal(out=both, in_=total[:, 2 * pair : 2 * pair + 2])
+            if holds_factor(pair):
+                nc.vector.tensor_scalar(out=both, in0=both, scalar1=1024.0, scalar2=None, op0=ALU.mult)
+
+        def divide(r):
+            row = rows[r][:, 0 : P * (r + 1)]
+            scale = inverse[:, r : r + 1]
+            if r in DIVIDED_ON_SCALAR:
+                nc.scalar.activation(out=row, in_=row, func=ACT.Copy, scale=scale)
+            elif holds_factor(r // 2):
+                nc.vector.tensor_scalar(out=row, in0=row, scalar1=scale, scalar2=None, op0=ALU.mult)
+            else:
+                nc.vector.tensor_scalar(out=row, in0=row, scalar1=scale, scalar2=1024.0, op0=ALU.mult, op1=ALU.mult)
+            nc.sync.dma_start(out=out[0, P * r : P * (r + 1), 0 : P * (r + 1)], in_=row)
+
+        widen(3, range(0, 8, 2), "vector")
+        widen(3, range(1, 8, 2), "scalar")
         turn("k", 0)
-        widen(3, "v")
-        copy_out("k", 0)
-        zab = psum.tile([P, P], BF16, name="zab", tag="Z", bufs=3)
-        nc.tensor.transpose(zab[:], ab_rows[:], ident_b[:])
-        nc.scalar.copy(out=ab[:], in_=zab[:, 0:8])
-        quant(0)
-        permute_weights(0)
-        permute_scales(0, nc.vector)
-        turn("k", 1)
-        copy_out("k", 1)
-        m1(0)
-        m1(1)
-        widen(2, "v")
-        act1(0)
-        quant(1)
-        act1(1)
-        m1(2)
-        permute_weights(1)
-        permute_scales(1, nc.gpsimd)
-        for i in range(7):
-            wid = P * (i + 1)
-            nc.sync.dma_start(out=out[0, P * i : P * (i + 1), wid:S], in_=zeros[:, 0 : S - wid])
-        m1(3)
-        m2(0, 0)
-        m2(0, 1)
-        turn("k", 2)
-        copy_out("k", 2)
-        turn("k", 3)
-        copy_out("k", 3, "v")
-        act1(2)
-        act1(3)
-        quant(2)
-        m1(4)
-        m1(5)
-        widen(1, "v")
+        widen(2, range(0, 5), "vector")
+        widen(2, range(5, 8), "scalar")
+        permute_codes(0)
+        copy_out("k", 0, "vector")
+        turn_factors()
         turn("q", 3)
+        permute_scales(0, nc.vector)
+        quantise(0)
         copy_out("q", 3)
+        turn("k", 1)
+        permute_codes(1)
+        copy_out("k", 1)
         turn("q", 2)
+        project_first(0)
+        widen(1, range(0, 4), "vector")
+        widen(1, range(4, 5), "scalar")
         copy_out("q", 2)
-        quant(3)
-        widen(0, "v")
-        UNITS = {0: [4, 5], 1: [6, 7], 2: [8, 9], 3: [10, 11], 4: [12, 13], 5: [14, 15], 6: [], 7: []}
-        for p in range(8):
-            done = rows_of(p - 1)
-            closing = rows_of(p - 2)
-            if p == 1:
-                turn("q", 1)
-                copy_out("q", 1)
-                turn("q", 0)
-                copy_out("q", 0)
-                quant(4)
-            if closing:
-                mask_and_sum(closing[0])
-            prod(p, 0)
-            m2(p + 1, 0)
-            if closing:
-                mask_and_sum(closing[1])
-            if p:
-                fquant(p - 1)
-            for i in UNITS[p]:
-                act1(i)
-                m1(i + 2)
-            if done:
-                zrow(done[0])
-                squares(done[0])
-            if closing:
-                invert(closing[1] // 2)
-            prod(p, 1)
-            m2(p + 1, 1)
-            if done:
-                zrow(done[1])
-                squares(done[1])
-            if closing:
-                normalise(closing[0])
-                normalise(closing[1])
-        fquant(7, 1, 2)
-        zrow(1)
-        squares(1)
-        fquant(7, 0, 1)
-        zrow(0)
-        squares(0)
+        quantise(1)
+        permute_scales(1, nc.gpsimd)
+        turn("k", 2)
+        widen(1, range(5, 8), "vector")
+        scale_first(0)
+        project_first(1)
+        copy_out("k", 2, "vector")
+        widen(0, range(7, 8), "scalar")
+        scale_first(1)
+        turn("k", 3)
+        quantise(3)
+        project_first(2)
+        widen(0, range(0, 1), "vector")
+        copy_out("k", 3, "vector")
+        widen(0, range(6, 7), "scalar")
+        project_first(3)
+        scale_first(2)
+        project_second(0, 0)
+        project_second(0, 1)
+        widen(0, range(1, 3), "vector")
+        quantise(2)
+        scale_first(3)
+        turn("q", 1)
+
+        def refill(n):
+            if n + 2 < len(first_banks):
+                project_first(n + 2)
+
+        multiply(0, 0)
+        copy_out("q", 1)
+        project_first(4)
+        multiply(0, 1)
+        project_first(5)
+        scale_first(4)
+        refill(4)
+        widen(0, range(3, 6), "vector")
+        project_second(1, 0)
+        scale_first(5)
+        quantise_features(0)
+        project_second(1, 1)
+        multiply(1, 0)
+        scale_first(6)
+        project_first(7)
+        multiply(1, 1)
+        turn("q", 0)
+        scale_first(7)
+        project_first(8)
+        project_second(2, 0)
+        project_first(9)
+        quantise_features(1)
+        copy_out("q", 0)
+        for n, banks in ((2, (8, 9, 10)), (3, (11, 12)), (4, (13, 14, 15))):
+            multiply(n, 0)
+            scale_first(banks[0])
+            project_second(n, 1)
+            refill(banks[0])
+            if n == 2:
+                quantise(4)
+            else:
+                quantise_features(n - 1)
+            multiply(n, 1)
+            scale_first(banks[1])
+            project_second(n + 1, 0)
+            refill(banks[1])
+            for i in banks[2:]:
+                scale_first(i)
+                refill(i)
+
+        multiply(5, 0)
+        project_second(5, 1)
+        quantise_features(4)
+        multiply(5, 1)
+        project_second(6, 0)
+        product(0)
+        product(1)
+        multiply(6, 0)
+        square(0)
+        product(2)
+        quantise_features(5)
+        project_second(6, 1)
+        multiply(6, 1)
+        project_second(7, 0)
+        product(3)
+        square(1)
+        multiply(7, 0)
+        square(2)
+        product(4)
+        quantise_features(6)
+        project_second(7, 1)
+        mask_and_sum(7)
+        product(5)
+        square(3)
+        multiply(7, 1)
+        square(4)
+        product(6)
+        mask_and_sum(6)
+        quantise_features(7, (1,))
+        product(7)
+        quantise_features(7, (0,))
+        square(5)
+        invert(3)
+        square(6)
+        mask_and_sum(5)
+        product(8)
+        divide(7)
+        square(7)
+        product(9)
+        square(8)
+        mask_and_sum(4)
+        product(10)
+        divide(6)
+        product(11)
+        invert(2)
         mask_and_sum(3)
+        square(9)
+        divide(4)
+        divide(5)
         mask_and_sum(2)
+        square(10)
         invert(1)
+        square(11)
         mask_and_sum(1)
-        times_1024(1)
         mask_and_sum(0)
-        normalise(3, "s")
+        divide(3)
+        divide(2)
         invert(0)
-        normalise(2, factor=False)
-        normalise(1)
-        normalise(0)
+        divide(1)
+        divide(0)

import concourse.mybir as mybir
from concourse.masks import make_identity

S, D, R = 1024, 512, 512
P = 128
PAIR = 2 * P
BANK = 512
PACK = 4
RUN = 8

F32 = mybir.dt.float32
BF16 = mybir.dt.bfloat16
I32 = mybir.dt.int32
U32 = mybir.dt.uint32
U8 = mybir.dt.uint8
FP8 = mybir.dt.float8_e4m3fn
FP8X4 = mybir.dt.float8_e4m3fn_x4
ALU = mybir.AluOpType
ACT = mybir.ActivationFunctionType

GROUPS = [("k", (0,)), ("k", (1,)), ("k", (2, 3)), ("q", (2, 3)), ("q", (0, 1))]
ORDER = [("k", 0), ("k", 1), ("k", 2), ("k", 3), ("q", 3), ("q", 2), ("q", 1), ("q", 0)]
DIVIDED_ON_SCALAR = (4, 3)

FLOPS = 4 * 2 * S * D * R + 2 * R * (S * (S + 1) // 2)


def tile_polysketchdegreefourcausalweights_d1p_kernel(
    tc, q_bytes, q_scale, k, g1_words, g1_scales, g2_words, g2_scales, a, b, out
):
    nc = tc.nc
    with tc.tile_pool(name="keep", bufs=1) as keep, tc.psum_pool(name="banks", bufs=2) as psum, tc.manual_schedule():

        def sb(name, shape, dtype):
            return keep.tile(shape, dtype, name=name, align_bytes=64)

        def bank(name, tag, bufs):
            return psum.tile([P, BANK], F32, name=name, tag=tag, bufs=bufs)

        identity = sb("identity", [P, P], F32)
        identity_bf = sb("identity_bf", [P, P], BF16)
        mask = sb("mask", [P, P + 3], F32)
        zeros = sb("zeros", [P, S - P], F32)
        factor_rows = sb("factor_rows", [P, P], BF16)
        factors = sb("factors", [P, 2 * PACK], F32)
        scale_rows = [sb("scale_rows%d" % i, [P, P], I32) for i in range(2)]
        words = [sb("words%d" % i, [P, R], I32) for i in range(2)]
        w_scales = [sb("w_scales%d" % i, [P, P], I32) for i in range(2)]
        w_codes = [sb("w_codes%d" % i, [P, R], I32) for i in range(2)]
        k_raw = [sb("k_raw%d" % i, [P, 2 * D], BF16) for i in range(4)]
        q_raw = [sb("q_raw%d" % i, [P, 2, 2 * D], U8) for i in range(2)]
        q_scales = sb("q_scales", [P, 4, 8], F32)
        q_bf = [sb("q_bf%d" % i, [P, 2 * D], BF16) for i in range(4)]
        widths = [PAIR * len(pairs) for kind, pairs in GROUPS]
        grouped = [sb("grouped%d" % i, [P, PACK * n], BF16) for i, n in enumerate(widths)]
        codes = [sb("codes%d" % i, [P, n], U32) for i, n in enumerate(widths)]
        scales = [sb("scales%d" % i, [P, n], U8) for i, n in enumerate(widths)]
        first = [sb("first%d" % i, [P, PACK, n], F32) for i, n in enumerate(widths)]
        feature = {pair: sb("feature_%s%d" % pair, [P, PACK * PAIR], BF16) for pair in ORDER}
        fk_codes = sb("fk_codes", [P, S], U32)
        fk_scales = sb("fk_scales", [P, S], U8)
        fq_codes = [sb("fq_codes%d" % i, [P, PAIR], U32) for i in range(4)]
        fq_scales = [sb("fq_scales%d" % i, [P, PAIR], U8) for i in range(4)]
        rows = [sb("rows%d" % r, [P, P * (r + 1) + 3], F32) for r in range(8)]
        total = sb("total", [P, 8], F32)
        inverse = sb("inverse", [P, 8], F32)

        nc.vector.memset(scale_rows[0][:], 0)
        nc.vector.memset(factor_rows[:], 0.0)
        nc.vector.memset(scale_rows[1][:], 0)
        nc.vector.memset(mask[:], 1.0)
        nc.vector.memset(zeros[:], 0.0)
        for r in range(8):
            nc.vector.memset(rows[r][:, P * (r + 1) : P * (r + 1) + 1], 512.0 * 1024.0)
        make_identity(nc, identity[:])

        k_view = k[0].rearrange("(i p j) d -> p i (j d)", p=P, j=2)
        q_view = q_bytes[0].rearrange("(i p j) d -> p i (j d)", p=P, j=2)

        def load_scale_rows(i, src):
            view = src[0].bitcast(I32).rearrange("(q s) n -> s q n", s=4)
            for s in range(4):
                nc.sync.dma_start(out=scale_rows[i][s : P : 32, :], in_=view[s])

        def load_words(i, src):
            nc.sync.dma_start(out=words[i][:], in_=src[0].rearrange("p n t -> p (n t)").bitcast(I32))

        def load_factor(row, src):
            nc.gpsimd.dma_start(
                out=factor_rows[row : row + PACK, :].rearrange("t (c r) -> t c r", r=RUN),
                in_=src.rearrange("(c t r) -> t c r", t=PACK, r=RUN),
            )

        def load_q(half):
            nc.sync.dma_start(out=q_raw[half][:], in_=q_view[:, 2 * half : 2 * half + 2, :])

        def load_k(pair):
            nc.sync.dma_start(out=k_raw[pair][:], in_=k_view[:, pair, :])

        load_factor(0, b)
        load_factor(PACK, a)
        nc.gpsimd.affine_select(
            out=mask[:, 0:P], in_=mask[:, 0:P], pattern=[[-1, P]], compare_op=ALU.is_ge, fill=0.0, base=0, channel_multiplier=1
        )
        nc.sync.dma_start(out=q_scales[:], in_=q_scale[0].rearrange("(i p j) c -> p i (j c)", p=P, j=2))
        load_q(1)
        load_k(0)
        load_words(0, g1_words)
        load_scale_rows(0, g1_scales)
        load_k(1)
        load_words(1, g2_words)
        load_q(0)
        load_k(2)
        load_scale_rows(1, g2_scales)
        load_k(3)
        for r in range(7):
            width = P * (r + 1)
            nc.sync.dma_start(out=out[0, P * r : P * (r + 1), width:S], in_=zeros[:, 0 : S - width])

        nc.scalar.copy(out=identity_bf[:], in_=identity[:])

        place = {}
        for g, (kind, pairs) in enumerate(GROUPS):
            for n, pair in enumerate(pairs):
                place[kind, pair] = (g, PAIR * n)
        held = {}

        def turn_factors():
            z = psum.tile([P, P], BF16, name="turned_factors", tag="Z", bufs=3)
            nc.tensor.transpose(z[:], factor_rows[:], identity_bf[:])
            nc.scalar.copy(out=factors[:], in_=z[:, 0 : 2 * PACK])

        def permute_codes(i):
            nc.vector.tensor_copy(
                out=w_codes[i][:].rearrange("p (t c r) -> p t c r", t=PACK, r=RUN),
                in_=words[i][:].rearrange("p (c t r) -> p t c r", t=PACK, r=RUN),
            )

        def permute_scales(i, engine):
            engine.tensor_copy(
                out=w_scales[i][:].rearrange("p (t c r) -> p t c r", t=PACK, r=RUN // 4),
                in_=scale_rows[i][:].rearrange("p (c t r) -> p t c r", t=PACK, r=RUN // 4),
            )

        def widen(pair, blocks, engine):
            for n in blocks:
                cols = slice(P * n, P * (n + 1))
                src = q_raw[pair // 2][:, pair % 2, cols].bitcast(FP8)
                dst = q_bf[pair][:, cols]
                scale = q_scales[:, pair, n : n + 1]
                if engine == "vector":
                    nc.vector.tensor_scalar(out=dst, in0=src, scalar1=scale, scalar2=None, op0=ALU.mult)
                else:
                    nc.scalar.activation(out=dst, in_=src, func=ACT.Copy, scale=scale)

        def turn(kind, pair):
            pairs_of_bf = (q_bf if kind == "q" else k_raw)[pair][:].bitcast(F32)
            z = bank("turned_%s%d" % (kind, pair), "Z", 3)
            for j in range(2):
                for u in range(2):
                    nc.tensor.transpose(
                        z[:, PAIR * u + P * j : PAIR * u + P * (j + 1)],
                        pairs_of_bf[:, PAIR * j + u : PAIR * (j + 1) : 2],
                        identity[:],
                    )
            held["turned", kind, pair] = z

        def copy_out(kind, pair, engine="scalar"):
            g, c0 = place[kind, pair]
            dst = grouped[g][:, PACK * c0 : PACK * (c0 + PAIR)].bitcast(F32).rearrange("p (c j u) -> p c j u", j=2, u=2)
            src = held["turned", kind, pair][:].rearrange("p (u j c) -> p c j u", u=2, j=2)
            if engine == "scalar":
                nc.scalar.copy(out=dst, in_=src)
            else:
                nc.vector.tensor_copy(out=dst, in_=src)

        def quantise(g):
            nc.vector.quantize_mx(out=codes[g][:].bitcast(FP8X4), scales=scales[g][:], in_=grouped[g][:])

        def project(dst, i, t, g, c0, c1):
            nc.tensor.matmul_mx(
                out=dst,
                lhsT=w_codes[i][:, P * t : P * (t + 1)].bitcast(FP8X4),
                lhsT_scale=w_scales[i][:].bitcast(U8)[:, P * t : P * (t + 1)],
                rhs=codes[g][:, c0:c1].bitcast(FP8X4),
                rhs_scale=scales[g][:, c0:c1],
                start=True,
                stop=True,
            )

        first_banks = []
        for g, n in enumerate(widths):
            for t in range(0, PACK, BANK // n):
                first_banks.append((g, t, BANK // n))

        def project_first(n):
            g, t0, count = first_banks[n]
            z = bank("first_bank%d" % n, "A", 3)
            for e in range(count):
                project(z[:, widths[g] * e : widths[g] * (e + 1)], 0, t0 + e, g, 0, widths[g])
            held["first", n] = z

        def scale_first(n):
            g, t0, count = first_banks[n]
            column = PACK if GROUPS[g][0] == "q" else 0
            for e in range(count):
                nc.scalar.activation(
                    out=first[g][:, t0 + e, :],
                    in_=held["first", n][:, widths[g] * e : widths[g] * (e + 1)],
                    func=ACT.Copy,
                    scale=factors[:, column + t0 + e : column + t0 + e + 1],
                )

        def project_second(n, half):
            g, c0 = place[ORDER[n]]
            z = bank("second_bank%d_%d" % (n, half), "B", 2)
            for t in range(PACK):
                project(z[:, P * t : P * (t + 1)], 1, t, g, c0 + P * half, c0 + P * (half + 1))
            held["second", n, half] = z

        def multiply(n, half):
            g, c0 = place[ORDER[n]]
            nc.vector.tensor_tensor(
                out=feature[ORDER[n]][:, BANK * half : BANK * (half + 1)].rearrange("p (c i t) -> p c t i", i=4, t=PACK),
                in0=held["second", n, half][:].rearrange("p (t c i) -> p c t i", t=PACK, i=4),
                in1=first[g][:, :, c0 + P * half : c0 + P * (half + 1)].rearrange("p t (c i) -> p c t i", i=4),
                op=ALU.mult,
            )

        def quantise_features(n, halves=(0, 1)):
            kind, pair = ORDER[n]
            c0, c1 = P * halves[0], P * (halves[-1] + 1)
            src = feature[ORDER[n]][:, PACK * c0 : PACK * c1]
            if kind == "q":
                dst, dst_scales = fq_codes[pair][:, c0:c1], fq_scales[pair][:, c0:c1]
            else:
                cols = slice(PAIR * pair + c0, PAIR * pair + c1)
                dst, dst_scales = fk_codes[:, cols], fk_scales[:, cols]
            nc.vector.quantize_mx(out=dst.bitcast(FP8X4), scales=dst_scales, in_=src)

        parts = [(r, h) for r in range(7, -1, -1) for h in range((r + 4) // 4)]

        def product(n):
            r, h = parts[n]
            rows_of_pair = slice(P * (r % 2), P * (r % 2 + 1))
            z = bank("z%d_%d" % (r, h), "Z", 3)
            c0, end = BANK * h, min(P * (r + 1), BANK * (h + 1))
            c = c0
            while c < end:
                step = max(m for m in (512, 256, 128) if c + m <= end)
                nc.tensor.matmul_mx(
                    out=z[:, c - c0 : c - c0 + step],
                    lhsT=fq_codes[r // 2][:, rows_of_pair].bitcast(FP8X4),
                    lhsT_scale=fq_scales[r // 2][:, rows_of_pair],
                    rhs=fk_codes[:, c : c + step].bitcast(FP8X4),
                    rhs_scale=fk_scales[:, c : c + step],
                    start=True,
                    stop=True,
                )
                c += step
            held["z", r, h] = z

        def square(n):
            r, h = parts[n]
            diagonal = P * r
            c0, end = BANK * h, min(P * (r + 1), BANK * (h + 1))
            left = min(end, diagonal)
            if left > c0:
                sums = P * (r + 1) + 1 + h
                nc.scalar.activation(
                    out=rows[r][:, c0:left], in_=held["z", r, h][:, 0 : left - c0], func=ACT.Square, accum_out=rows[r][:, sums : sums + 1]
                )
            if end > diagonal:
                nc.scalar.activation(out=rows[r][:, diagonal:end], in_=held["z", r, h][:, diagonal - c0 : end - c0], func=ACT.Square)

        def mask_and_sum(r):
            part = rows[r][:, P * r : P * (r + 1) + 1 + (r + 3) // 4]
            nc.vector.scalar_tensor_tensor(
                out=part,
                in0=part,
                scalar=1.0,
                in1=mask[:, 0 : P + 1 + (r + 3) // 4],
                op0=ALU.mult,
                op1=ALU.mult,
                accum_out=total[:, r : r + 1],
            )

        def holds_factor(pair):
            return any(r // 2 == pair for r in DIVIDED_ON_SCALAR)

        def invert(pair):
            both = inverse[:, 2 * pair : 2 * pair + 2]
            nc.vector.reciprocal(out=both, in_=total[:, 2 * pair : 2 * pair + 2])
            if holds_factor(pair):
                nc.vector.tensor_scalar(out=both, in0=both, scalar1=1024.0, scalar2=None, op0=ALU.mult)

        def divide(r):
            row = rows[r][:, 0 : P * (r + 1)]
            scale = inverse[:, r : r + 1]
            if r in DIVIDED_ON_SCALAR:
                nc.scalar.activation(out=row, in_=row, func=ACT.Copy, scale=scale)
            elif holds_factor(r // 2):
                nc.vector.tensor_scalar(out=row, in0=row, scalar1=scale, scalar2=None, op0=ALU.mult)
            else:
                nc.vector.tensor_scalar(out=row, in0=row, scalar1=scale, scalar2=1024.0, op0=ALU.mult, op1=ALU.mult)
            nc.sync.dma_start(out=out[0, P * r : P * (r + 1), 0 : P * (r + 1)], in_=row)

        widen(3, range(0, 8, 2), "vector")
        widen(3, range(1, 8, 2), "scalar")
        turn("k", 0)
        widen(2, range(0, 5), "vector")
        widen(2, range(5, 8), "scalar")
        permute_codes(0)
        copy_out("k", 0, "vector")
        turn_factors()
        turn("q", 3)
        permute_scales(0, nc.vector)
        quantise(0)
        copy_out("q", 3)
        turn("k", 1)
        permute_codes(1)
        copy_out("k", 1)
        turn("q", 2)
        project_first(0)
        widen(1, range(0, 4), "vector")
        widen(1, range(4, 5), "scalar")
        copy_out("q", 2)
        quantise(1)
        permute_scales(1, nc.gpsimd)
        turn("k", 2)
        widen(1, range(5, 8), "vector")
        scale_first(0)
        project_first(1)
        copy_out("k", 2, "vector")
        widen(0, range(7, 8), "scalar")
        scale_first(1)
        turn("k", 3)
        quantise(3)
        project_first(2)
        widen(0, range(0, 1), "vector")
        copy_out("k", 3, "vector")
        widen(0, range(6, 7), "scalar")
        project_first(3)
        scale_first(2)
        project_second(0, 0)
        project_second(0, 1)
        widen(0, range(1, 3), "vector")
        quantise(2)
        scale_first(3)
        turn("q", 1)

        def refill(n):
            if n + 2 < len(first_banks):
                project_first(n + 2)

        multiply(0, 0)
        copy_out("q", 1)
        project_first(4)
        multiply(0, 1)
        project_first(5)
        scale_first(4)
        refill(4)
        widen(0, range(3, 6), "vector")
        project_second(1, 0)
        scale_first(5)
        quantise_features(0)
        project_second(1, 1)
        multiply(1, 0)
        scale_first(6)
        project_first(7)
        multiply(1, 1)
        turn("q", 0)
        scale_first(7)
        project_first(8)
        project_second(2, 0)
        project_first(9)
        quantise_features(1)
        copy_out("q", 0)
        for n, banks in ((2, (8, 9, 10)), (3, (11, 12)), (4, (13, 14, 15))):
            multiply(n, 0)
            scale_first(banks[0])
            project_second(n, 1)
            refill(banks[0])
            if n == 2:
                quantise(4)
            else:
                quantise_features(n - 1)
            multiply(n, 1)
            scale_first(banks[1])
            project_second(n + 1, 0)
            refill(banks[1])
            for i in banks[2:]:
                scale_first(i)
                refill(i)

        multiply(5, 0)
        project_second(5, 1)
        quantise_features(4)
        multiply(5, 1)
        project_second(6, 0)
        product(0)
        product(1)
        multiply(6, 0)
        square(0)
        product(2)
        quantise_features(5)
        project_second(6, 1)
        multiply(6, 1)
        project_second(7, 0)
        product(3)
        square(1)
        multiply(7, 0)
        square(2)
        product(4)
        quantise_features(6)
        project_second(7, 1)
        mask_and_sum(7)
        product(5)
        square(3)
        multiply(7, 1)
        square(4)
        product(6)
        mask_and_sum(6)
        quantise_features(7, (1,))
        product(7)
        quantise_features(7, (0,))
        square(5)
        invert(3)
        square(6)
        mask_and_sum(5)
        product(8)
        divide(7)
        square(7)
        product(9)
        square(8)
        mask_and_sum(4)
        product(10)
        divide(6)
        product(11)
        invert(2)
        mask_and_sum(3)
        square(9)
        divide(4)
        divide(5)
        mask_and_sum(2)
        square(10)
        invert(1)
        square(11)
        mask_and_sum(1)
        mask_and_sum(0)
        divide(3)
        divide(2)
        invert(0)
        divide(1)
        divide(0)
